import numpy as np
import ml_dtypes


def mxq(x, axis, fmt="e4m3"):
    dtype, down = {"e4m3": (ml_dtypes.float8_e4m3fn, 7), "e5m2": (ml_dtypes.float8_e5m2, 14)}[fmt]
    v = np.moveaxis(np.asarray(x, np.float32).astype(ml_dtypes.bfloat16).astype(np.float64), axis, -1)
    blocks = v.reshape(v.shape[:-1] + (-1, 32))
    amax = np.abs(blocks).max(-1, keepdims=True)
    byte = np.maximum(np.where(amax > 0, np.frexp(amax)[1] - 1 + 127, 0) - down, 1)
    scale = np.exp2(byte - 127.0)
    codes = (blocks / scale).astype(np.float32).astype(dtype).astype(np.float64)
    return np.moveaxis((codes * scale).reshape(v.shape), -1, axis)


WIDE = False


def mx_kscale(k):
    if not WIDE:
        return np.ones(k)
    levels = np.array([10, -10, 5, -5, 0])
    if k % 512:
        return np.exp2(np.random.permutation(np.resize(levels, k // 32))).repeat(32)
    a = np.empty((k // 512, 16))
    for p in range(k // 512):
        a[p, :8] = np.random.permutation(np.resize(levels, 8))
        for g in range(8):
            far = levels[np.abs(levels - a[p, g]) >= 10]
            a[p, g + 8] = far[np.random.randint(len(far))]
    return np.exp2(a.ravel()).repeat(32)


BF16 = ml_dtypes.bfloat16


def bf(x):
    return np.asarray(x, np.float32).astype(BF16)


def f64(x):
    return np.asarray(x).astype(np.float64)


E2M1 = np.array([0.0, 0.5, 1.0, 1.5, 2.0, 3.0, 4.0, 6.0, -0.0, -0.5, -1.0, -1.5, -2.0, -3.0, -4.0, -6.0])


def pack_weight(w, fmt):
    k, n = w.shape
    w = f64(bf(w)).reshape(k // 32, 32, n)
    amax = np.abs(w).max(1)
    if fmt == "e4m3":
        byte = np.frexp(amax)[1] - 1 + 127 - 7
    else:
        mant, ex = np.frexp(amax / 6.0)
        byte = np.where(mant > 0.5, ex, ex - 1) + 127
    byte = np.clip(np.where(amax > 0, byte, 1), 1, 254)
    scaled = (w * np.exp2(127.0 - byte)[:, None, :]).reshape(k, n).astype(np.float32)
    by_word = np.ascontiguousarray(scaled.reshape(k // 512, 128, 4, n).transpose(0, 1, 3, 2))
    if fmt == "e4m3":
        words = by_word.astype(ml_dtypes.float8_e4m3fn).view(np.uint8)
    else:
        c = by_word.astype(ml_dtypes.float4_e2m1fn).view(np.uint8) & 0xF
        words = c[..., 0::2] | (c[..., 1::2] << 4)
    return np.ascontiguousarray(words), np.ascontiguousarray(byte.astype(np.uint8).reshape(k // 512, 16, n))


def unpack_weight(words, scales, fmt):
    g, p, n, _ = words.shape
    if fmt == "e4m3":
        vals = np.ascontiguousarray(words).view(ml_dtypes.float8_e4m3fn).astype(np.float64)
    else:
        nib = np.empty((g, p, n, 4), np.uint8)
        nib[..., 0::2] = words & 0xF
        nib[..., 1::2] = words >> 4
        vals = E2M1[nib]
    vals = vals * np.repeat(np.exp2(scales.astype(np.float64) - 127.0), 8, axis=1)[..., None]
    return vals.transpose(0, 1, 3, 2).reshape(g * 512, n)
def pack4(w):
    words, scales = pack_weight(w, "e2m1")
    return words.reshape(words.shape[0], 128, -1), scales


def unpack4(words, scales):
    return unpack_weight(words.reshape(words.shape[0], 128, -1, 2), scales, "e2m1")


V, B, F = 1024, 2048, 1024


def setup_inputs():
    s = mx_kscale(V)
    t = mx_kscale(B)
    system = np.random.standard_normal((B, V)) ** 4 / (3.0 * V)
    image = np.exp(0.7 * np.random.standard_normal((V, F)))
    a_words, a_scales = pack4(system.T * s[:, None])
    x_words, x_scales = pack4(image / s[:, None])
    back_words, back_scales = pack_weight(system / t[:, None], "e4m3")
    return {"a_words": a_words, "a_scales": a_scales,
            "x_words": x_words, "x_scales": x_scales,
            "back_words": back_words, "back_scales": back_scales,
            "y": bf(np.random.exponential(1.2, (B, F)) * t[:, None]),
            "r": bf(0.2 + 0.3 * np.random.random_sample(B)),
            "img": bf(image),
            "sens": bf(system.sum(axis=0))}


def reference(a_words, a_scales, x_words, x_scales, back_words, back_scales, y, r, img, sens):
    a = unpack4(a_words, a_scales)
    x = unpack4(x_words, x_scales)
    back = unpack_weight(back_words, back_scales, "e4m3")
    expected = (a.T @ x) + f64(r)[:, None]
    ratio = f64(y) / expected
    corr = back.T @ mxq(ratio, 0, "e4m3")
    return f64(img) * corr / f64(sens)[:, None]

@@ -1,0 +1,240 @@
+from contextlib import ExitStack
+
+import concourse.mybir as mybir
+from concourse.masks import make_identity
+
+V, B, F = 1024, 2048, 1024
+FLOPS = 2 * V * B * F * 2
+
+F32 = mybir.dt.float32
+BF16 = mybir.dt.bfloat16
+U32 = mybir.dt.uint32
+I32 = mybir.dt.int32
+U8 = mybir.dt.uint8
+FP8X4 = mybir.dt.float8_e4m3fn_x4
+FP4X4 = mybir.dt.float4_e2m1fn_x4
+ACT = mybir.ActivationFunctionType
+ALU = mybir.AluOpType
+
+P = 128
+NG = 4
+NM = 8
+BANK = 512
+W = 256
+NCH = F // W
+
+
+def tile_mlem_pet_update_s4_kernel(tc, a_words, a_scales, x_words, x_scales, back_words, back_scales, y, r, img, sens, out):
+    nc = tc.nc
+    with ExitStack() as ctx:
+        keep = ctx.enter_context(tc.tile_pool(name="keep", bufs=1))
+        work = ctx.enter_context(tc.tile_pool(name="work", bufs=3))
+        psum = ctx.enter_context(tc.psum_pool(name="psum", bufs=4))
+        ctx.enter_context(tc.manual_schedule())
+
+        x_sb = [keep.tile([P, 2, 1024], U8, name="x_sb%d" % h, align_bytes=256) for h in range(2)]
+        xs = keep.tile([P, 2, 1024], U8, name="xs", align_bytes=256)
+        a_raw = [keep.tile([P, 2, 2048], U8, name="a_raw%d" % h, align_bytes=256) for h in range(2)]
+        as_raw = keep.tile([P, 2, 2048], U8, name="as_raw", align_bytes=256)
+        a_perm = [keep.tile([P, 2, 4, 256], U8, name="a_perm%d" % g, align_bytes=256) for g in range(NG)]
+        as_perm = [keep.tile([P, 2, 4, 128], U8, name="as_perm%d" % g, align_bytes=256) for g in range(NG)]
+        back_sb = [keep.tile([P, 4096], U8, name="back%d" % g, align_bytes=256) for g in range(NG)]
+        bs = keep.tile([P, 1024], U8, name="bs", align_bytes=256)
+        y_sb = [[keep.tile([P, 4, 512], BF16, name="y%d_%d" % (g, h), align_bytes=256) for h in range(2)] for g in range(NG)]
+        img_sb = [keep.tile([P, NM, 512], BF16, name="img%d" % h, align_bytes=256) for h in range(2)]
+        r_sb = keep.tile([P, 4, 4], BF16, name="r_sb")
+        sens_rows = keep.tile([P, P], BF16, name="sens_rows", align_bytes=256)
+        ident = keep.tile([P, P], BF16, name="ident", align_bytes=256)
+        rsens = keep.tile([P, NM], F32, name="rsens")
+        warm = keep.tile([P, 1], F32, name="warm")
+        warm_out = keep.tile([P, 1], F32, name="warm_out")
+
+        def load_a(h):
+            nc.sync.dma_start(out=a_raw[h][:].bitcast(I32), in_=a_words[:, :, 2048 * h : 2048 * h + 2048].rearrange("g p b -> p g b").bitcast(I32))
+
+        def load_x(h, queue):
+            queue.dma_start(out=x_sb[h][:].bitcast(I32), in_=x_words[:, :, 1024 * h : 1024 * h + 1024].rearrange("g p b -> p g b").bitcast(I32))
+
+        def load_scales(tile, src, q, queue):
+            queue.dma_start(out=tile[32 * q : 32 * q + 4, :, :].bitcast(I32), in_=src[:, 4 * q : 4 * q + 4, :].rearrange("g r n -> r g n").bitcast(I32))
+
+        def load_y(g, h):
+            nc.sync.dma_start(out=y_sb[g][h][:], in_=y.rearrange("(g p t) f -> g p t f", p=P, t=4)[g][:, :, 512 * h : 512 * h + 512])
+
+        def load_back(g):
+            nc.sync.dma_start(out=back_sb[g][:].bitcast(I32), in_=back_words[g].rearrange("p n t -> p (n t)").bitcast(I32))
+
+        def load_img(h):
+            nc.sync.dma_start(out=img_sb[h][:], in_=img.rearrange("(m p) f -> p m f", p=P)[:, :, 512 * h : 512 * h + 512])
+
+        nc.vector.memset(as_raw[:].rearrange("p g n -> p (g n)").bitcast(I32), 0)
+        nc.gpsimd.memset(xs[:].rearrange("p g n -> p (g n)").bitcast(I32), 0)
+        nc.vector.memset(warm[:], 1.0)
+        nc.scalar.activation(out=warm_out[:], in_=warm[:], func=ACT.Abs_reciprocal_sqrt)
+        load_a(0)
+        load_x(0, nc.sync)
+        for q in range(4):
+            load_scales(as_raw, a_scales, q, nc.sync)
+        for q in range(4):
+            load_scales(xs, x_scales, q, nc.sync)
+        nc.sync.dma_start(out=r_sb[:], in_=r.rearrange("(g p t) -> p g t", p=P, t=4))
+        nc.gpsimd.memset(sens_rows[:], 0.0)
+        nc.gpsimd.memset(bs[:].bitcast(I32), 0)
+        make_identity(nc, ident[:])
+        load_a(1)
+        load_y(0, 0)
+        load_y(1, 0)
+        nc.sync.dma_start(out=sens_rows[0:NM, :], in_=sens.rearrange("(m p) -> m p", p=P))
+        for q in range(4):
+            nc.sync.dma_start(out=bs[32 * q : 32 * q + 16, :].bitcast(I32), in_=back_scales[:, 4 * q : 4 * q + 4, :].bitcast(I32))
+        load_back(0)
+        load_y(2, 0)
+        load_back(1)
+        load_y(3, 0)
+        load_back(2)
+        load_back(3)
+        load_img(0)
+        load_x(1, nc.sync)
+        for g in range(NG):
+            load_y(g, 1)
+        load_img(1)
+
+        def permute_codes(g):
+            for k in range(2):
+                nc.vector.tensor_copy(
+                    out=a_perm[g][:, k].rearrange("p t (c b) -> p t c b", b=2),
+                    in_=a_raw[g // 2][:, k, 1024 * (g % 2) : 1024 * (g % 2) + 1024].rearrange("p (c t b) -> p t c b", t=4, b=2),
+                )
+
+        def permute_scales(g):
+            nc.vector.tensor_copy(out=as_perm[g][:], in_=as_raw[:, :, 512 * g : 512 * g + 512].rearrange("p k (c t) -> p k t c", t=4))
+
+        tiles1 = {}
+        u = {}
+        rec = {}
+        codes = {}
+        planes = {}
+        quant_in = {}
+
+        def stage1(j, half):
+            c, g = divmod(j, NG)
+            h, off = divmod(W * c, 512)
+            bank = psum.tile([P, 2, W], F32, name="bank", tag="s1", bufs=3)
+            for e in range(2):
+                t = 2 * half + e
+                tiles1[j, t] = bank[:, e, :]
+                for k in range(2):
+                    nc.tensor.matmul_mx(
+                        out=bank[:, e, :],
+                        lhsT=a_perm[g][:, k, t, :].bitcast(FP4X4),
+                        lhsT_scale=as_perm[g][:, k, t, :],
+                        rhs=x_sb[h][:, k, 2 * off : 2 * off + 2 * W].bitcast(FP4X4),
+                        rhs_scale=xs[:, k, W * c : W * c + W],
+                        start=(k == 0),
+                        stop=(k == 1),
+                    )
+
+        def inverse_root(j, t):
+            g = j % NG
+            if t == 0:
+                u[j] = work.tile([P, 4, W], F32, name="u", align_bytes=256)
+            nc.scalar.activation(out=u[j][:, t, :], in_=tiles1[j, t], func=ACT.Abs_reciprocal_sqrt, bias=r_sb[:, g, t : t + 1])
+
+        LASTJ = NCH * NG - 1
+
+        def parts(j):
+            n = 1 if j == LASTJ else 1
+            return [(i * W // n, (i + 1) * W // n) for i in range(n)]
+
+        def square(j, on_vector):
+            rec[j] = work.tile([P, 4, W], F32, name="rec", align_bytes=256)
+            for lo, hi in parts(j):
+                if on_vector:
+                    nc.vector.tensor_tensor(out=rec[j][:, :, lo:hi], in0=u[j][:, :, lo:hi], in1=u[j][:, :, lo:hi], op=ALU.mult)
+                else:
+                    nc.scalar.activation(out=rec[j][:, :, lo:hi], in_=u[j][:, :, lo:hi], func=ACT.Square)
+
+        def ratio(j):
+            c, g = divmod(j, NG)
+            h, off = divmod(W * c, 512)
+            quant_in[j] = work.tile([P, 4 * W], BF16, name="quant_in", align_bytes=256)
+            for lo, hi in parts(j):
+                nc.vector.tensor_tensor(
+                    out=quant_in[j][:, 4 * lo : 4 * hi].rearrange("p (c i t) -> p c t i", i=4, t=4),
+                    in0=rec[j][:, :, lo:hi].rearrange("p t (c i) -> p c t i", i=4),
+                    in1=y_sb[g][h][:, :, off + lo : off + hi].rearrange("p t (c i) -> p c t i", i=4),
+                    op=ALU.mult,
+                )
+
+        def quantize(j):
+            codes[j] = keep.tile([P, W], U32, name="codes%d" % j, align_bytes=256)
+            planes[j] = keep.tile([P, W], U8, name="plane%d" % j, align_bytes=256)
+            for lo, hi in parts(j):
+                nc.vector.quantize_mx(out=codes[j][:, lo:hi].bitcast(FP8X4), scales=planes[j][:, lo:hi], in_=quant_in[j][:, 4 * lo : 4 * hi])
+
+        accs = {}
+
+        def stage2_pass(m, c, g):
+            nc.tensor.matmul_mx(
+                out=accs[c, m],
+                lhsT=back_sb[g][:, 512 * m : 512 * m + 512].bitcast(FP8X4),
+                lhsT_scale=bs[4 * g : P, P * m : P * m + P],
+                rhs=codes[NG * c + g][:].bitcast(FP8X4),
+                rhs_scale=planes[NG * c + g][:],
+                start=(g == 0),
+                stop=(g == NG - 1),
+            )
+
+        res = {}
+        nacc = []
+
+        def finish(c, m):
+            h, off = divmod(W * c, 512)
+            if (c, m // 2) not in res:
+                res[c, m // 2] = work.tile([P, 2, W], F32, name="res", align_bytes=256, bufs=4)
+                res[c, m // 2, "n"] = 0
+            pix = img_sb[h][:, m, off : off + W]
+            nc.vector.scalar_tensor_tensor(out=res[c, m // 2][:, m % 2, :], in0=accs[c, m], scalar=rsens[:, m : m + 1], in1=pix, op0=ALU.mult, op1=ALU.mult)
+            res[c, m // 2, "n"] += 1
+            if res[c, m // 2, "n"] == 2:
+                m = m // 2 * 2
+                nc.sync.dma_start(out=out.rearrange("(m p) f -> p m f", p=P)[:, m : m + 2, W * c : W * c + W], in_=res[c, m // 2][:])
+
+        last = NCH * NG
+        LC = NCH - 1
+        permute_codes(0)
+        permute_scales(0)
+        permute_scales(1)
+        permute_codes(1)
+        permute_scales(2)
+        permute_scales(3)
+        permute_codes(2)
+        permute_codes(3)
+
+        SEQ = [("T", "S1", 0, 0), ("T", "S1", 0, 1), ("S", "R", 0, 0), ("S", "R", 0, 1), ("T", "S1", 1, 0), ("S", "R", 0, 2), ("S", "R", 0, 3), ("T", "S1", 1, 1), ("S", "R", 1, 0), ("S", "R", 1, 1), ("S", "R", 1, 2), ("T", "S1", 2, 0), ("S", "R", 1, 3), ("S", "SQ", 0), ("T", "S1", 2, 1), ("V", "SQ", 1), ("T", "S1", 3, 0), ("S", "R", 2, 0), ("S", "R", 2, 1), ("V", "TT", 0), ("S", "R", 2, 2), ("T", "S1", 3, 1), ("S", "R", 2, 3), ("S", "R", 3, 0), ("T", "S1", 4, 0), ("V", "TT", 1), ("S", "R", 3, 1), ("S", "R", 3, 2), ("T", "S1", 4, 1), ("S", "R", 3, 3), ("S", "SQ", 2), ("V", "Q", 0), ("T", "S1", 5, 0), ("V", "Q", 1), ("V", "SQ", 3), ("T", "P", 0, 0, 0), ("T", "P", 0, 0, 1), ("T", "P", 0, 1, 0), ("S", "R", 4, 0), ("T", "P", 0, 1, 1), ("T", "P", 0, 2, 0), ("S", "R", 4, 1), ("T", "P", 0, 2, 1), ("T", "P", 0, 3, 0), ("V", "TT", 2), ("T", "P", 0, 3, 1), ("S", "R", 4, 2), ("T", "P", 0, 4, 0), ("T", "S1", 5, 1), ("S", "R", 4, 3), ("S", "R", 5, 0), ("T", "S1", 6, 0), ("S", "R", 5, 1), ("V", "TT", 3), ("S", "R", 5, 2), ("T", "P", 0, 4, 1), ("T", "S1", 6, 1), ("S", "R", 5, 3), ("S", "SQ", 4), ("T", "S1", 7, 0), ("V", "Q", 2), ("V", "Q", 3), ("T", "P", 0, 0, 2), ("V", "SQ", 5), ("T", "P", 0, 1, 2), ("T", "P", 0, 2, 2), ("S", "R", 6, 0), ("T", "P", 0, 3, 2), ("T", "P", 0, 4, 2), ("S", "R", 6, 1), ("T", "P", 0, 0, 3), ("T", "P", 0, 1, 3), ("S", "R", 6, 2), ("T", "P", 0, 2, 3), ("V", "TT", 4), ("T", "S1", 7, 1), ("S", "R", 6, 3), ("S", "R", 7, 0), ("T", "P", 0, 3, 3), ("T", "S1", 8, 0), ("S", "R", 7, 1), ("V", "TT", 5), ("S", "R", 7, 2), ("T", "S1", 8, 1), ("S", "R", 7, 3), ("S", "SQ", 6), ("T", "P", 0, 4, 3), ("T", "S1", 9, 0), ("V", "Q", 4), ("V", "Q", 5), ("V", "E", 0, 0), ("S", "R", 8, 0), ("V", "TT", 6), ("T", "P", 0, 5, 0), ("S", "R", 8, 1), ("T", "P", 0, 5, 1), ("T", "P", 0, 5, 2), ("S", "R", 8, 2), ("T", "P", 0, 5, 3), ("T", "S1", 9, 1), ("S", "R", 8, 3), ("V", "E", 0, 1), ("S", "SQ", 7), ("T", "S1", 10, 0), ("V", "Q", 6), ("V", "E", 0, 2), ("T", "P", 0, 6, 0), ("V", "E", 0, 3), ("T", "P", 0, 6, 1), ("T", "P", 0, 6, 2), ("S", "R", 9, 0), ("V", "E", 0, 4), ("T", "P", 0, 6, 3), ("T", "P", 0, 7, 0), ("V", "TT", 7), ("S", "R", 9, 1), ("T", "P", 0, 7, 1), ("T", "P", 0, 7, 2), ("T", "P", 0, 7, 3), ("S", "R", 9, 2), ("T", "P", 1, 0, 0), ("T", "S1", 10, 1), ("S", "R", 9, 3), ("S", "SQ", 8), ("V", "E", 0, 5), ("T", "S1", 11, 0), ("V", "Q", 7), ("V", "E", 0, 6), ("T", "P", 1, 0, 1), ("T", "P", 1, 0, 2), ("V", "E", 0, 7), ("T", "P", 1, 0, 3), ("S", "R", 10, 0), ("T", "P", 1, 1, 0), ("V", "TT", 8), ("T", "P", 1, 1, 1), ("S", "R", 10, 1), ("T", "P", 1, 1, 2), ("T", "P", 1, 1, 3), ("S", "R", 10, 2), ("T", "P", 1, 2, 0), ("T", "S1", 11, 1), ("S", "R", 10, 3), ("V", "E", 1, 0), ("S", "SQ", 9), ("T", "P", 1, 2, 1), ("T", "S1", 12, 0), ("V", "Q", 8), ("V", "E", 1, 1), ("T", "P", 1, 2, 2), ("V", "SQ", 10), ("T", "P", 1, 2, 3), ("T", "P", 1, 3, 0), ("S", "R", 11, 0), ("T", "P", 1, 3, 1), ("T", "P", 1, 3, 2), ("S", "R", 11, 1), ("T", "P", 1, 3, 3), ("T", "P", 1, 4, 0), ("S", "R", 11, 2), ("T", "P", 1, 4, 1), ("V", "TT", 9), ("T", "S1", 12, 1), ("S", "R", 11, 3), ("S", "R", 12, 0), ("T", "S1", 13, 0), ("S", "R", 12, 1), ("V", "TT", 10), ("S", "R", 12, 2), ("T", "P", 1, 4, 2), ("T", "S1", 13, 1), ("S", "R", 12, 3), ("S", "SQ", 11), ("T", "P", 1, 4, 3), ("T", "S1", 14, 0), ("V", "Q", 9), ("V", "Q", 10), ("T", "P", 1, 5, 0), ("T", "P", 1, 5, 1), ("V", "E", 1, 2), ("S", "R", 13, 0), ("T", "P", 1, 5, 2), ("T", "P", 1, 5, 3), ("V", "TT", 11), ("T", "P", 1, 6, 0), ("S", "R", 13, 1), ("T", "P", 1, 6, 1), ("T", "P", 1, 6, 2), ("S", "R", 13, 2), ("T", "P", 1, 6, 3), ("T", "S1", 14, 1), ("S", "R", 13, 3), ("V", "E", 1, 3), ("S", "SQ", 12), ("T", "S1", 15, 0), ("V", "Q", 11), ("V", "E", 1, 4), ("T", "P", 1, 7, 0), ("V", "E", 1, 5), ("T", "P", 1, 7, 1), ("T", "P", 1, 7, 2), ("S", "R", 14, 0), ("V", "E", 1, 6), ("T", "P", 1, 7, 3), ("T", "P", 2, 0, 0), ("S", "R", 14, 1), ("V", "TT", 12), ("T", "P", 2, 0, 1), ("T", "P", 2, 0, 2), ("S", "R", 14, 2), ("T", "P", 2, 0, 3), ("T", "S1", 15, 1), ("S", "R", 14, 3), ("S", "SQ", 13), ("T", "P", 2, 1, 0), ("V", "E", 1, 7), ("T", "P", 2, 1, 1), ("T", "P", 2, 1, 2), ("V", "Q", 12), ("T", "P", 2, 1, 3), ("T", "P", 2, 2, 0), ("V", "E", 2, 0), ("T", "P", 2, 2, 1), ("T", "P", 2, 2, 2), ("V", "E", 2, 1), ("T", "P", 2, 2, 3), ("S", "R", 15, 0), ("T", "P", 2, 3, 0), ("V", "TT", 13), ("T", "P", 2, 3, 1), ("S", "R", 15, 1), ("T", "P", 2, 3, 2), ("T", "P", 2, 3, 3), ("S", "R", 15, 2), ("T", "P", 2, 4, 0), ("T", "P", 2, 4, 1), ("S", "R", 15, 3), ("T", "P", 2, 4, 2), ("T", "P", 2, 4, 3), ("T", "P", 2, 5, 0), ("S", "SQ", 14), ("V", "E", 2, 2), ("T", "P", 2, 5, 1), ("T", "P", 2, 5, 2), ("V", "Q", 13), ("T", "P", 2, 5, 3), ("T", "P", 2, 6, 0), ("V", "E", 2, 3), ("T", "P", 2, 6, 1), ("T", "P", 2, 6, 2), ("V", "E", 2, 4), ("T", "P", 2, 6, 3), ("S", "SQ", 15), ("T", "P", 2, 7, 0), ("V", "E", 2, 5), ("T", "P", 2, 7, 1), ("T", "P", 2, 7, 2), ("V", "TT", 14), ("T", "P", 2, 7, 3), ("T", "P", 3, 0, 0), ("T", "P", 3, 0, 1), ("T", "P", 3, 1, 0), ("T", "P", 3, 1, 1), ("T", "P", 3, 2, 0), ("T", "P", 3, 2, 1), ("T", "P", 3, 3, 0), ("V", "TT", 15), ("T", "P", 3, 3, 1), ("T", "P", 3, 4, 0), ("T", "P", 3, 4, 1), ("T", "P", 3, 5, 0), ("T", "P", 3, 5, 1), ("V", "Q", 14), ("V", "Q", 15), ("T", "P", 3, 0, 2), ("T", "P", 3, 1, 2), ("V", "E", 2, 6), ("T", "P", 3, 2, 2), ("T", "P", 3, 3, 2), ("V", "E", 2, 7), ("T", "P", 3, 4, 2), ("T", "P", 3, 5, 2), ("T", "P", 3, 0, 3), ("T", "P", 3, 1, 3), ("V", "E", 3, 0), ("T", "P", 3, 2, 3), ("T", "P", 3, 3, 3), ("V", "E", 3, 1), ("T", "P", 3, 4, 3), ("T", "P", 3, 5, 3), ("V", "E", 3, 2), ("T", "P", 3, 6, 0), ("T", "P", 3, 6, 1), ("V", "E", 3, 3), ("T", "P", 3, 6, 2), ("T", "P", 3, 6, 3), ("V", "E", 3, 4), ("T", "P", 3, 7, 0), ("T", "P", 3, 7, 1), ("V", "E", 3, 5), ("T", "P", 3, 7, 2), ("T", "P", 3, 7, 3), ("V", "E", 3, 6), ("V", "E", 3, 7)]
+        nsq = 0
+        for ev in SEQ:
+            e, kind, args = ev[0], ev[1], ev[2:]
+            if kind == "S1":
+                if args == (1, 0):
+                    turned = psum.tile([P, P], BF16, name="turned", tag="acc", bufs=5)
+                    nc.tensor.transpose(turned[:], sens_rows[:], ident[:])
+                    nc.vector.reciprocal(out=rsens[:], in_=turned[:, 0:NM])
+                stage1(*args)
+            elif kind == "P":
+                c, m, g = args
+                if g == 0:
+                    late = len(nacc) >= NCH * NM - 3
+                    accs[c, m] = psum.tile([P, BANK], F32, name="acc", tag=("s1" if late else "acc"), bufs=(3 if late else 5))[:, 0:W]
+                    nacc.append(m)
+                stage2_pass(m, c, g)
+            elif kind == "R":
+                inverse_root(*args)
+            elif kind == "SQ":
+                square(args[0], e == "V")
+            elif kind == "TT":
+                ratio(args[0])
+            elif kind == "Q":
+                quantize(args[0])
+            else:
+                finish(*args)

@@ -20,8 +20,9 @@ P = 128
 NG = 4
 NM = 8
 BANK = 512
-W = 256
-NCH = F // W
+WIDTHS = [512,256,256]
+STARTS = [sum(WIDTHS[:i]) for i in range(len(WIDTHS))]
+NCH = len(WIDTHS)
 
 
 def tile_mlem_pet_update_s4_kernel(tc, a_words, a_scales, x_words, x_scales, back_words, back_scales, y, r, img, sens, out):
@@ -34,7 +35,7 @@ def tile_mlem_pet_update_s4_kernel(tc, a_words, a_scales, x_words, x_scales, bac
 
         x_sb = [keep.tile([P, 2, 1024], U8, name="x_sb%d" % h, align_bytes=256) for h in range(2)]
         xs = keep.tile([P, 2, 1024], U8, name="xs", align_bytes=256)
-        a_raw = [keep.tile([P, 2, 2048], U8, name="a_raw%d" % h, align_bytes=256) for h in range(2)]
+        a_raw = [keep.tile([P, 2, 2048], U8, name="a_raw%d" % g, align_bytes=256) for g in range(2)]
         as_raw = keep.tile([P, 2, 2048], U8, name="as_raw", align_bytes=256)
         a_perm = [keep.tile([P, 2, 4, 256], U8, name="a_perm%d" % g, align_bytes=256) for g in range(NG)]
         as_perm = [keep.tile([P, 2, 4, 128], U8, name="as_perm%d" % g, align_bytes=256) for g in range(NG)]
@@ -49,8 +50,9 @@ def tile_mlem_pet_update_s4_kernel(tc, a_words, a_scales, x_words, x_scales, bac
         warm = keep.tile([P, 1], F32, name="warm")
         warm_out = keep.tile([P, 1], F32, name="warm_out")
 
-        def load_a(h):
-            nc.sync.dma_start(out=a_raw[h][:].bitcast(I32), in_=a_words[:, :, 2048 * h : 2048 * h + 2048].rearrange("g p b -> p g b").bitcast(I32))
+        def load_a(lo, hi, queue):
+            if lo % 2 == 0:
+                queue.dma_start(out=a_raw[lo // 2][:].bitcast(I32), in_=a_words[:, :, 1024 * lo : 1024 * lo + 2048].rearrange("g p b -> p g b").bitcast(I32))
 
         def load_x(h, queue):
             queue.dma_start(out=x_sb[h][:].bitcast(I32), in_=x_words[:, :, 1024 * h : 1024 * h + 1024].rearrange("g p b -> p g b").bitcast(I32))
@@ -67,21 +69,23 @@ def tile_mlem_pet_update_s4_kernel(tc, a_words, a_scales, x_words, x_scales, bac
         def load_img(h):
             nc.sync.dma_start(out=img_sb[h][:], in_=img.rearrange("(m p) f -> p m f", p=P)[:, :, 512 * h : 512 * h + 512])
 
+        load_x(0, nc.gpsimd)
         nc.vector.memset(as_raw[:].rearrange("p g n -> p (g n)").bitcast(I32), 0)
-        nc.gpsimd.memset(xs[:].rearrange("p g n -> p (g n)").bitcast(I32), 0)
-        nc.vector.memset(warm[:], 1.0)
-        nc.scalar.activation(out=warm_out[:], in_=warm[:], func=ACT.Abs_reciprocal_sqrt)
-        load_a(0)
-        load_x(0, nc.sync)
-        for q in range(4):
+        nc.vector.memset(xs[:].rearrange("p g n -> p (g n)").bitcast(I32), 0)
+        load_scales(as_raw, a_scales, 0, nc.sync)
+        load_scales(as_raw, a_scales, 1, nc.sync)
+        load_a(0, 2, nc.sync)
+        for q in (2, 3):
             load_scales(as_raw, a_scales, q, nc.sync)
         for q in range(4):
             load_scales(xs, x_scales, q, nc.sync)
         nc.sync.dma_start(out=r_sb[:], in_=r.rearrange("(g p t) -> p g t", p=P, t=4))
+        load_a(2, 4, nc.sync)
+        nc.vector.memset(warm[:], 1.0)
+        nc.scalar.activation(out=warm_out[:], in_=warm[:], func=ACT.Abs_reciprocal_sqrt)
         nc.gpsimd.memset(sens_rows[:], 0.0)
         nc.gpsimd.memset(bs[:].bitcast(I32), 0)
         make_identity(nc, ident[:])
-        load_a(1)
         load_y(0, 0)
         load_y(1, 0)
         nc.sync.dma_start(out=sens_rows[0:NM, :], in_=sens.rearrange("(m p) -> m p", p=P))
@@ -91,23 +95,35 @@ def tile_mlem_pet_update_s4_kernel(tc, a_words, a_scales, x_words, x_scales, bac
         load_y(2, 0)
         load_back(1)
         load_y(3, 0)
+        load_x(1, nc.sync)
         load_back(2)
         load_back(3)
         load_img(0)
-        load_x(1, nc.sync)
         for g in range(NG):
             load_y(g, 1)
         load_img(1)
-
-        def permute_codes(g):
+        def permute_codes(g, ts=(0, 4)):
+            lo, hi = ts
             for k in range(2):
                 nc.vector.tensor_copy(
-                    out=a_perm[g][:, k].rearrange("p t (c b) -> p t c b", b=2),
-                    in_=a_raw[g // 2][:, k, 1024 * (g % 2) : 1024 * (g % 2) + 1024].rearrange("p (c t b) -> p t c b", t=4, b=2),
+                    out=a_perm[g][:, k, lo:hi].rearrange("p t (c b) -> p t c b", b=2),
+                    in_=a_raw[g // 2][:, k, 1024 * (g % 2) : 1024 * (g % 2) + 1024].rearrange("p (c t b) -> p t c b", t=4, b=2)[:, lo:hi],
                 )
 
-        def permute_scales(g):
-            nc.vector.tensor_copy(out=as_perm[g][:], in_=as_raw[:, :, 512 * g : 512 * g + 512].rearrange("p k (c t) -> p k t c", t=4))
+        def permute_scales(g, ts=(0, 4)):
+            lo, hi = ts
+            nc.vector.tensor_copy(out=as_perm[g][:, :, lo:hi], in_=as_raw[:, :, 512 * g : 512 * g + 512].rearrange("p k (c t) -> p k t c", t=4)[:, :, lo:hi])
+
+        permute_codes(0, (0, 2))
+        permute_scales(0, (0, 2))
+        permute_codes(0, (2, 4))
+        permute_scales(0, (2, 4))
+        permute_scales(1)
+        permute_codes(1)
+        permute_scales(2)
+        permute_scales(3)
+        permute_codes(2)
+        permute_codes(3)
 
         tiles1 = {}
         u = {}
@@ -116,38 +132,41 @@ def tile_mlem_pet_update_s4_kernel(tc, a_words, a_scales, x_words, x_scales, bac
         planes = {}
         quant_in = {}
 
-        def stage1(j, half):
+        def stage1(j, b, k_bank):
             c, g = divmod(j, NG)
-            h, off = divmod(W * c, 512)
-            bank = psum.tile([P, 2, W], F32, name="bank", tag="s1", bufs=3)
-            for e in range(2):
-                t = 2 * half + e
+            w = WIDTHS[c]
+            h, off = divmod(STARTS[c], 512)
+            per = BANK // w
+            bank = psum.tile([P, per, w], F32, name="bank%d" % k_bank, bufs=1)
+            for e in range(per):
+                t = per * b + e
                 tiles1[j, t] = bank[:, e, :]
                 for k in range(2):
                     nc.tensor.matmul_mx(
                         out=bank[:, e, :],
                         lhsT=a_perm[g][:, k, t, :].bitcast(FP4X4),
                         lhsT_scale=as_perm[g][:, k, t, :],
-                        rhs=x_sb[h][:, k, 2 * off : 2 * off + 2 * W].bitcast(FP4X4),
-                        rhs_scale=xs[:, k, W * c : W * c + W],
+                        rhs=x_sb[h][:, k, 2 * off : 2 * off + 2 * w].bitcast(FP4X4),
+                        rhs_scale=xs[:, k, STARTS[c] : STARTS[c] + w],
                         start=(k == 0),
                         stop=(k == 1),
                     )
 
         def inverse_root(j, t):
-            g = j % NG
+            c, g = divmod(j, NG)
             if t == 0:
-                u[j] = work.tile([P, 4, W], F32, name="u", align_bytes=256)
+                u[j] = work.tile([P, 4, WIDTHS[c]], F32, name="u", align_bytes=256)
             nc.scalar.activation(out=u[j][:, t, :], in_=tiles1[j, t], func=ACT.Abs_reciprocal_sqrt, bias=r_sb[:, g, t : t + 1])
 
         LASTJ = NCH * NG - 1
 
         def parts(j):
             n = 1 if j == LASTJ else 1
-            return [(i * W // n, (i + 1) * W // n) for i in range(n)]
+            w = WIDTHS[j // NG]
+            return [(i * w // n, (i + 1) * w // n) for i in range(n)]
 
         def square(j, on_vector):
-            rec[j] = work.tile([P, 4, W], F32, name="rec", align_bytes=256)
+            rec[j] = work.tile([P, 4, WIDTHS[j // NG]], F32, name="rec", align_bytes=256)
             for lo, hi in parts(j):
                 if on_vector:
                     nc.vector.tensor_tensor(out=rec[j][:, :, lo:hi], in0=u[j][:, :, lo:hi], in1=u[j][:, :, lo:hi], op=ALU.mult)
@@ -156,19 +175,23 @@ def tile_mlem_pet_update_s4_kernel(tc, a_words, a_scales, x_words, x_scales, bac
 
         def ratio(j):
             c, g = divmod(j, NG)
-            h, off = divmod(W * c, 512)
-            quant_in[j] = work.tile([P, 4 * W], BF16, name="quant_in", align_bytes=256)
+            w = WIDTHS[c]
+            quant_in[j] = work.tile([P, 4 * w], BF16, name="quant_in", align_bytes=256)
             for lo, hi in parts(j):
-                nc.vector.tensor_tensor(
-                    out=quant_in[j][:, 4 * lo : 4 * hi].rearrange("p (c i t) -> p c t i", i=4, t=4),
-                    in0=rec[j][:, :, lo:hi].rearrange("p t (c i) -> p c t i", i=4),
-                    in1=y_sb[g][h][:, :, off + lo : off + hi].rearrange("p t (c i) -> p c t i", i=4),
-                    op=ALU.mult,
-                )
+                for a in range(lo, hi, 512):
+                    h, off = divmod(STARTS[c] + a, 512)
+                    n = min(hi - a, 512 - off)
+                    nc.vector.tensor_tensor(
+                        out=quant_in[j][:, 4 * a : 4 * (a + n)].rearrange("p (c i t) -> p c t i", i=4, t=4),
+                        in0=rec[j][:, :, a : a + n].rearrange("p t (c i) -> p c t i", i=4),
+                        in1=y_sb[g][h][:, :, off : off + n].rearrange("p t (c i) -> p c t i", i=4),
+                        op=ALU.mult,
+                    )
 
         def quantize(j):
-            codes[j] = keep.tile([P, W], U32, name="codes%d" % j, align_bytes=256)
-            planes[j] = keep.tile([P, W], U8, name="plane%d" % j, align_bytes=256)
+            w = WIDTHS[j // NG]
+            codes[j] = keep.tile([P, w], U32, name="codes%d" % j, align_bytes=256)
+            planes[j] = keep.tile([P, w], U8, name="plane%d" % j, align_bytes=256)
             for lo, hi in parts(j):
                 nc.vector.quantize_mx(out=codes[j][:, lo:hi].bitcast(FP8X4), scales=planes[j][:, lo:hi], in_=quant_in[j][:, 4 * lo : 4 * hi])
 
@@ -186,47 +209,34 @@ def tile_mlem_pet_update_s4_kernel(tc, a_words, a_scales, x_words, x_scales, bac
             )
 
         res = {}
-        nacc = []
 
         def finish(c, m):
-            h, off = divmod(W * c, 512)
-            if (c, m // 2) not in res:
-                res[c, m // 2] = work.tile([P, 2, W], F32, name="res", align_bytes=256, bufs=4)
-                res[c, m // 2, "n"] = 0
-            pix = img_sb[h][:, m, off : off + W]
-            nc.vector.scalar_tensor_tensor(out=res[c, m // 2][:, m % 2, :], in0=accs[c, m], scalar=rsens[:, m : m + 1], in1=pix, op0=ALU.mult, op1=ALU.mult)
-            res[c, m // 2, "n"] += 1
-            if res[c, m // 2, "n"] == 2:
-                m = m // 2 * 2
-                nc.sync.dma_start(out=out.rearrange("(m p) f -> p m f", p=P)[:, m : m + 2, W * c : W * c + W], in_=res[c, m // 2][:])
+            w = WIDTHS[c]
+            h, off = divmod(STARTS[c], 512)
+            single = w == 512 or (c == NCH - 1 and m >= 6)
+            n = 1 if single else 2
+            key = (c, m // n)
+            if key not in res:
+                res[key] = [work.tile([P, n, w], F32, name="res%d" % n, align_bytes=256, bufs=(8 if n == 2 else 8)), 0]
+            tile = res[key][0]
+            nc.vector.scalar_tensor_tensor(out=tile[:, m % n, :], in0=accs[c, m], scalar=rsens[:, m : m + 1], in1=img_sb[h][:, m, off : off + w], op0=ALU.mult, op1=ALU.mult)
+            res[key][1] += 1
+            if res[key][1] == n:
+                m = m // n * n
+                nc.sync.dma_start(out=out.rearrange("(m p) f -> p m f", p=P)[:, m : m + n, STARTS[c] : STARTS[c] + w], in_=tile[:])
 
-        last = NCH * NG
-        LC = NCH - 1
-        permute_codes(0)
-        permute_scales(0)
-        permute_scales(1)
-        permute_codes(1)
-        permute_scales(2)
-        permute_scales(3)
-        permute_codes(2)
-        permute_codes(3)
-
-        SEQ = [("T", "S1", 0, 0), ("T", "S1", 0, 1), ("S", "R", 0, 0), ("S", "R", 0, 1), ("T", "S1", 1, 0), ("S", "R", 0, 2), ("S", "R", 0, 3), ("T", "S1", 1, 1), ("S", "R", 1, 0), ("S", "R", 1, 1), ("S", "R", 1, 2), ("T", "S1", 2, 0), ("S", "R", 1, 3), ("S", "SQ", 0), ("T", "S1", 2, 1), ("V", "SQ", 1), ("T", "S1", 3, 0), ("S", "R", 2, 0), ("S", "R", 2, 1), ("V", "TT", 0), ("S", "R", 2, 2), ("T", "S1", 3, 1), ("S", "R", 2, 3), ("S", "R", 3, 0), ("T", "S1", 4, 0), ("V", "TT", 1), ("S", "R", 3, 1), ("S", "R", 3, 2), ("T", "S1", 4, 1), ("S", "R", 3, 3), ("S", "SQ", 2), ("V", "Q", 0), ("T", "S1", 5, 0), ("V", "Q", 1), ("V", "SQ", 3), ("T", "P", 0, 0, 0), ("T", "P", 0, 0, 1), ("T", "P", 0, 1, 0), ("S", "R", 4, 0), ("T", "P", 0, 1, 1), ("T", "P", 0, 2, 0), ("S", "R", 4, 1), ("T", "P", 0, 2, 1), ("T", "P", 0, 3, 0), ("V", "TT", 2), ("T", "P", 0, 3, 1), ("S", "R", 4, 2), ("T", "P", 0, 4, 0), ("T", "S1", 5, 1), ("S", "R", 4, 3), ("S", "R", 5, 0), ("T", "S1", 6, 0), ("S", "R", 5, 1), ("V", "TT", 3), ("S", "R", 5, 2), ("T", "P", 0, 4, 1), ("T", "S1", 6, 1), ("S", "R", 5, 3), ("S", "SQ", 4), ("T", "S1", 7, 0), ("V", "Q", 2), ("V", "Q", 3), ("T", "P", 0, 0, 2), ("V", "SQ", 5), ("T", "P", 0, 1, 2), ("T", "P", 0, 2, 2), ("S", "R", 6, 0), ("T", "P", 0, 3, 2), ("T", "P", 0, 4, 2), ("S", "R", 6, 1), ("T", "P", 0, 0, 3), ("T", "P", 0, 1, 3), ("S", "R", 6, 2), ("T", "P", 0, 2, 3), ("V", "TT", 4), ("T", "S1", 7, 1), ("S", "R", 6, 3), ("S", "R", 7, 0), ("T", "P", 0, 3, 3), ("T", "S1", 8, 0), ("S", "R", 7, 1), ("V", "TT", 5), ("S", "R", 7, 2), ("T", "S1", 8, 1), ("S", "R", 7, 3), ("S", "SQ", 6), ("T", "P", 0, 4, 3), ("T", "S1", 9, 0), ("V", "Q", 4), ("V", "Q", 5), ("V", "E", 0, 0), ("S", "R", 8, 0), ("V", "TT", 6), ("T", "P", 0, 5, 0), ("S", "R", 8, 1), ("T", "P", 0, 5, 1), ("T", "P", 0, 5, 2), ("S", "R", 8, 2), ("T", "P", 0, 5, 3), ("T", "S1", 9, 1), ("S", "R", 8, 3), ("V", "E", 0, 1), ("S", "SQ", 7), ("T", "S1", 10, 0), ("V", "Q", 6), ("V", "E", 0, 2), ("T", "P", 0, 6, 0), ("V", "E", 0, 3), ("T", "P", 0, 6, 1), ("T", "P", 0, 6, 2), ("S", "R", 9, 0), ("V", "E", 0, 4), ("T", "P", 0, 6, 3), ("T", "P", 0, 7, 0), ("V", "TT", 7), ("S", "R", 9, 1), ("T", "P", 0, 7, 1), ("T", "P", 0, 7, 2), ("T", "P", 0, 7, 3), ("S", "R", 9, 2), ("T", "P", 1, 0, 0), ("T", "S1", 10, 1), ("S", "R", 9, 3), ("S", "SQ", 8), ("V", "E", 0, 5), ("T", "S1", 11, 0), ("V", "Q", 7), ("V", "E", 0, 6), ("T", "P", 1, 0, 1), ("T", "P", 1, 0, 2), ("V", "E", 0, 7), ("T", "P", 1, 0, 3), ("S", "R", 10, 0), ("T", "P", 1, 1, 0), ("V", "TT", 8), ("T", "P", 1, 1, 1), ("S", "R", 10, 1), ("T", "P", 1, 1, 2), ("T", "P", 1, 1, 3), ("S", "R", 10, 2), ("T", "P", 1, 2, 0), ("T", "S1", 11, 1), ("S", "R", 10, 3), ("V", "E", 1, 0), ("S", "SQ", 9), ("T", "P", 1, 2, 1), ("T", "S1", 12, 0), ("V", "Q", 8), ("V", "E", 1, 1), ("T", "P", 1, 2, 2), ("V", "SQ", 10), ("T", "P", 1, 2, 3), ("T", "P", 1, 3, 0), ("S", "R", 11, 0), ("T", "P", 1, 3, 1), ("T", "P", 1, 3, 2), ("S", "R", 11, 1), ("T", "P", 1, 3, 3), ("T", "P", 1, 4, 0), ("S", "R", 11, 2), ("T", "P", 1, 4, 1), ("V", "TT", 9), ("T", "S1", 12, 1), ("S", "R", 11, 3), ("S", "R", 12, 0), ("T", "S1", 13, 0), ("S", "R", 12, 1), ("V", "TT", 10), ("S", "R", 12, 2), ("T", "P", 1, 4, 2), ("T", "S1", 13, 1), ("S", "R", 12, 3), ("S", "SQ", 11), ("T", "P", 1, 4, 3), ("T", "S1", 14, 0), ("V", "Q", 9), ("V", "Q", 10), ("T", "P", 1, 5, 0), ("T", "P", 1, 5, 1), ("V", "E", 1, 2), ("S", "R", 13, 0), ("T", "P", 1, 5, 2), ("T", "P", 1, 5, 3), ("V", "TT", 11), ("T", "P", 1, 6, 0), ("S", "R", 13, 1), ("T", "P", 1, 6, 1), ("T", "P", 1, 6, 2), ("S", "R", 13, 2), ("T", "P", 1, 6, 3), ("T", "S1", 14, 1), ("S", "R", 13, 3), ("V", "E", 1, 3), ("S", "SQ", 12), ("T", "S1", 15, 0), ("V", "Q", 11), ("V", "E", 1, 4), ("T", "P", 1, 7, 0), ("V", "E", 1, 5), ("T", "P", 1, 7, 1), ("T", "P", 1, 7, 2), ("S", "R", 14, 0), ("V", "E", 1, 6), ("T", "P", 1, 7, 3), ("T", "P", 2, 0, 0), ("S", "R", 14, 1), ("V", "TT", 12), ("T", "P", 2, 0, 1), ("T", "P", 2, 0, 2), ("S", "R", 14, 2), ("T", "P", 2, 0, 3), ("T", "S1", 15, 1), ("S", "R", 14, 3), ("S", "SQ", 13), ("T", "P", 2, 1, 0), ("V", "E", 1, 7), ("T", "P", 2, 1, 1), ("T", "P", 2, 1, 2), ("V", "Q", 12), ("T", "P", 2, 1, 3), ("T", "P", 2, 2, 0), ("V", "E", 2, 0), ("T", "P", 2, 2, 1), ("T", "P", 2, 2, 2), ("V", "E", 2, 1), ("T", "P", 2, 2, 3), ("S", "R", 15, 0), ("T", "P", 2, 3, 0), ("V", "TT", 13), ("T", "P", 2, 3, 1), ("S", "R", 15, 1), ("T", "P", 2, 3, 2), ("T", "P", 2, 3, 3), ("S", "R", 15, 2), ("T", "P", 2, 4, 0), ("T", "P", 2, 4, 1), ("S", "R", 15, 3), ("T", "P", 2, 4, 2), ("T", "P", 2, 4, 3), ("T", "P", 2, 5, 0), ("S", "SQ", 14), ("V", "E", 2, 2), ("T", "P", 2, 5, 1), ("T", "P", 2, 5, 2), ("V", "Q", 13), ("T", "P", 2, 5, 3), ("T", "P", 2, 6, 0), ("V", "E", 2, 3), ("T", "P", 2, 6, 1), ("T", "P", 2, 6, 2), ("V", "E", 2, 4), ("T", "P", 2, 6, 3), ("S", "SQ", 15), ("T", "P", 2, 7, 0), ("V", "E", 2, 5), ("T", "P", 2, 7, 1), ("T", "P", 2, 7, 2), ("V", "TT", 14), ("T", "P", 2, 7, 3), ("T", "P", 3, 0, 0), ("T", "P", 3, 0, 1), ("T", "P", 3, 1, 0), ("T", "P", 3, 1, 1), ("T", "P", 3, 2, 0), ("T", "P", 3, 2, 1), ("T", "P", 3, 3, 0), ("V", "TT", 15), ("T", "P", 3, 3, 1), ("T", "P", 3, 4, 0), ("T", "P", 3, 4, 1), ("T", "P", 3, 5, 0), ("T", "P", 3, 5, 1), ("V", "Q", 14), ("V", "Q", 15), ("T", "P", 3, 0, 2), ("T", "P", 3, 1, 2), ("V", "E", 2, 6), ("T", "P", 3, 2, 2), ("T", "P", 3, 3, 2), ("V", "E", 2, 7), ("T", "P", 3, 4, 2), ("T", "P", 3, 5, 2), ("T", "P", 3, 0, 3), ("T", "P", 3, 1, 3), ("V", "E", 3, 0), ("T", "P", 3, 2, 3), ("T", "P", 3, 3, 3), ("V", "E", 3, 1), ("T", "P", 3, 4, 3), ("T", "P", 3, 5, 3), ("V", "E", 3, 2), ("T", "P", 3, 6, 0), ("T", "P", 3, 6, 1), ("V", "E", 3, 3), ("T", "P", 3, 6, 2), ("T", "P", 3, 6, 3), ("V", "E", 3, 4), ("T", "P", 3, 7, 0), ("T", "P", 3, 7, 1), ("V", "E", 3, 5), ("T", "P", 3, 7, 2), ("T", "P", 3, 7, 3), ("V", "E", 3, 6), ("V", "E", 3, 7)]
-        nsq = 0
+        SEQ = [("T", "S1", 0, 0, 0), ("T", "S1", 0, 1, 1), ("S", "R", 0, 0), ("T", "S1", 0, 2, 2), ("S", "R", 0, 1), ("T", "S1", 0, 3, 3), ("S", "R", 0, 2), ("T", "S1", 1, 0, 4), ("S", "R", 0, 3), ("T", "S1", 1, 1, 5), ("S", "R", 1, 0), ("T", "S1", 1, 2, 6), ("S", "R", 1, 1), ("T", "S1", 1, 3, 7), ("V", "SQ", 0), ("S", "R", 1, 2), ("T", "S1", 2, 0, 0), ("S", "R", 1, 3), ("T", "S1", 2, 1, 1), ("S", "R", 2, 0), ("T", "S1", 2, 2, 2), ("S", "R", 2, 1), ("T", "S1", 2, 3, 3), ("V", "TT", 0), ("S", "SQ", 1), ("T", "S1", 3, 0, 4), ("T", "S1", 3, 1, 5), ("T", "S1", 3, 2, 6), ("T", "S1", 3, 3, 7), ("S", "R", 2, 2), ("V", "Q", 0), ("T", "S1", 4, 0, 0), ("S", "R", 2, 3), ("V", "TT", 1), ("T", "S1", 4, 1, 1), ("S", "R", 3, 0), ("T", "P", 0, 0, 0, 2), ("T", "P", 0, 1, 0, 3), ("S", "R", 3, 1), ("T", "P", 0, 2, 0, 4), ("S", "SQ", 2), ("T", "P", 0, 3, 0, 5), ("V", "Q", 1), ("T", "P", 0, 0, 1), ("T", "P", 0, 1, 1), ("T", "P", 0, 2, 1), ("S", "R", 3, 2), ("V", "TT", 2), ("T", "P", 0, 3, 1), ("S", "R", 3, 3), ("T", "S1", 5, 0, 6), ("S", "R", 4, 0), ("T", "P", 0, 4, 0, 7), ("S", "R", 4, 1), ("T", "P", 0, 4, 1), ("S", "SQ", 3), ("T", "S1", 5, 1, 0), ("V", "Q", 2), ("T", "P", 0, 0, 2), ("T", "P", 0, 1, 2), ("T", "P", 0, 2, 2), ("S", "R", 4, 2), ("V", "TT", 3), ("T", "P", 0, 3, 2), ("S", "R", 4, 3), ("T", "P", 0, 4, 2), ("S", "R", 5, 0), ("T", "S1", 6, 0, 1), ("S", "R", 5, 1), ("S", "SQ", 4), ("T", "S1", 6, 1, 6), ("S", "R", 5, 2), ("V", "TT", 4), ("S", "R", 5, 3), ("S", "R", 6, 0), ("T", "S1", 7, 0, 0), ("S", "R", 6, 1), ("V", "Q", 3), ("S", "SQ", 5), ("T", "S1", 7, 1, 1), ("V", "Q", 4), ("T", "P", 0, 0, 3), ("T", "P", 0, 1, 3), ("S", "R", 6, 2), ("V", "E", 0, 0), ("T", "P", 0, 2, 3), ("S", "R", 6, 3), ("T", "P", 0, 3, 3), ("V", "TT", 5), ("S", "R", 7, 0), ("T", "S1", 8, 0, 2), ("S", "R", 7, 1), ("S", "SQ", 6), ("T", "S1", 8, 1, 6), ("V", "E", 0, 1), ("T", "P", 0, 4, 3), ("T", "P", 0, 5, 0, 0), ("V", "Q", 5), ("S", "R", 7, 2), ("T", "P", 0, 5, 1), ("V", "TT", 6), ("T", "P", 0, 5, 2), ("S", "R", 7, 3), ("T", "S1", 9, 0, 3), ("S", "R", 8, 0), ("S", "R", 8, 1), ("T", "S1", 9, 1, 1), ("S", "SQ", 7), ("V", "E", 0, 2), ("T", "P", 0, 5, 3), ("V", "Q", 6), ("T", "P", 0, 6, 0, 2), ("V", "E", 0, 3), ("T", "P", 0, 6, 1), ("S", "R", 8, 2), ("T", "P", 0, 6, 2), ("S", "R", 8, 3), ("V", "TT", 7), ("T", "S1", 10, 0, 4), ("S", "R", 9, 0), ("S", "R", 9, 1), ("T", "S1", 10, 1, 5), ("S", "SQ", 8), ("V", "E", 0, 4), ("T", "P", 0, 6, 3), ("T", "P", 0, 7, 0, 6), ("V", "Q", 7), ("T", "P", 0, 7, 1), ("S", "R", 9, 2), ("T", "P", 0, 7, 2), ("V", "E", 0, 5), ("S", "R", 9, 3), ("T", "S1", 11, 0, 3), ("S", "R", 10, 0), ("V", "TT", 8), ("T", "P", 0, 7, 3), ("S", "R", 10, 1), ("T", "S1", 11, 1, 7), ("S", "SQ", 9), ("T", "P", 1, 0, 0, 1), ("V", "E", 0, 6), ("T", "P", 1, 0, 1), ("T", "P", 1, 0, 2), ("T", "P", 1, 0, 3), ("T", "P", 1, 1, 0, 0), ("V", "Q", 8), ("S", "R", 10, 2), ("T", "P", 1, 1, 1), ("T", "P", 1, 1, 2), ("V", "TT", 9), ("S", "R", 10, 3), ("T", "P", 1, 1, 3), ("T", "P", 1, 2, 0, 4), ("S", "R", 11, 0), ("T", "P", 1, 2, 1), ("T", "P", 1, 2, 2), ("T", "P", 1, 2, 3), ("S", "R", 11, 1), ("T", "P", 1, 3, 0, 2), ("T", "P", 1, 3, 1), ("S", "SQ", 10), ("T", "P", 1, 3, 2), ("V", "E", 0, 7), ("T", "P", 1, 3, 3), ("T", "P", 1, 4, 0, 5), ("T", "P", 1, 4, 1), ("T", "P", 1, 4, 2), ("V", "Q", 9), ("T", "P", 1, 4, 3), ("T", "P", 1, 5, 0, 3), ("V", "E", 1, 0), ("S", "R", 11, 2), ("T", "P", 1, 5, 1), ("T", "P", 1, 5, 2), ("V", "TT", 10), ("T", "P", 1, 5, 3), ("S", "R", 11, 3), ("T", "P", 1, 6, 0, 6), ("T", "P", 1, 6, 1), ("T", "P", 1, 6, 2), ("T", "P", 1, 6, 3), ("S", "SQ", 11), ("T", "P", 1, 7, 0, 1), ("T", "P", 1, 7, 1), ("T", "P", 1, 7, 2), ("V", "E", 1, 1), ("T", "P", 1, 7, 3), ("T", "P", 2, 0, 0, 7), ("V", "Q", 10), ("T", "P", 2, 0, 1), ("T", "P", 2, 1, 0, 0), ("V", "E", 1, 2), ("T", "P", 2, 1, 1), ("T", "P", 2, 0, 2), ("T", "P", 2, 1, 2), ("V", "TT", 11), ("T", "P", 2, 2, 0, 4), ("T", "P", 2, 2, 1), ("T", "P", 2, 2, 2), ("V", "E", 1, 3), ("V", "Q", 11), ("T", "P", 2, 3, 0, 2), ("T", "P", 2, 3, 1), ("V", "E", 1, 4), ("T", "P", 2, 3, 2), ("T", "P", 2, 0, 3), ("V", "E", 1, 5), ("T", "P", 2, 1, 3), ("T", "P", 2, 2, 3), ("V", "E", 1, 6), ("T", "P", 2, 3, 3), ("T", "P", 2, 4, 0, 5), ("T", "P", 2, 4, 1), ("V", "E", 1, 7), ("T", "P", 2, 4, 2), ("T", "P", 2, 4, 3), ("V", "E", 2, 0), ("T", "P", 2, 5, 0, 3), ("T", "P", 2, 5, 1), ("V", "E", 2, 1), ("T", "P", 2, 5, 2), ("T", "P", 2, 5, 3), ("V", "E", 2, 2), ("T", "P", 2, 6, 0, 6), ("T", "P", 2, 6, 1), ("V", "E", 2, 3), ("T", "P", 2, 6, 2), ("T", "P", 2, 6, 3), ("T", "P", 2, 7, 0, 1), ("V", "E", 2, 4), ("T", "P", 2, 7, 1), ("T", "P", 2, 7, 2), ("V", "E", 2, 5), ("T", "P", 2, 7, 3), ("V", "E", 2, 6), ("V", "E", 2, 7)]
+        first = True
         for ev in SEQ:
             e, kind, args = ev[0], ev[1], ev[2:]
             if kind == "S1":
-                if args == (1, 0):
-                    turned = psum.tile([P, P], BF16, name="turned", tag="acc", bufs=5)
-                    nc.tensor.transpose(turned[:], sens_rows[:], ident[:])
-                    nc.vector.reciprocal(out=rsens[:], in_=turned[:, 0:NM])
                 stage1(*args)
             elif kind == "P":
-                c, m, g = args
+                c, m, g = args[:3]
+                if first:
+                    first = False
                 if g == 0:
-                    late = len(nacc) >= NCH * NM - 3
-                    accs[c, m] = psum.tile([P, BANK], F32, name="acc", tag=("s1" if late else "acc"), bufs=(3 if late else 5))[:, 0:W]
-                    nacc.append(m)
+                    accs[c, m] = psum.tile([P, BANK], F32, name="bank%d" % args[3], bufs=1)[:, 0 : WIDTHS[c]]
                 stage2_pass(m, c, g)
             elif kind == "R":
                 inverse_root(*args)
@@ -235,6 +245,11 @@ def tile_mlem_pet_update_s4_kernel(tc, a_words, a_scales, x_words, x_scales, bac
             elif kind == "TT":
                 ratio(args[0])
             elif kind == "Q":
+                if args[0] == 0:
+                    b0 = [ev2[5] for ev2 in SEQ if len(ev2) == 6][0]
+                    turned = psum.tile([P, P], BF16, name="bank%d" % b0, bufs=1)
+                    nc.tensor.transpose(turned[:], sens_rows[:], ident[:])
+                    nc.vector.reciprocal(out=rsens[:], in_=turned[:, 0:NM])
                 quantize(args[0])
             else:
                 finish(*args)

@@ -35,7 +35,8 @@ def tile_mlem_pet_update_s4_kernel(tc, a_words, a_scales, x_words, x_scales, bac
 
         x_sb = [keep.tile([P, 2, 1024], U8, name="x_sb%d" % h, align_bytes=256) for h in range(2)]
         xs = keep.tile([P, 2, 1024], U8, name="xs", align_bytes=256)
-        a_raw = [keep.tile([P, 2, 2048], U8, name="a_raw%d" % g, align_bytes=256) for g in range(2)]
+        a_late = keep.tile([P, 2, 2048], U8, name="a_late", align_bytes=256)
+        a_raw = [keep.tile([P, 2, 1024], U8, name="a_raw%d" % g, align_bytes=256) for g in range(2)] + [a_late[:, :, 0:1024], a_late[:, :, 1024:2048]]
         as_raw = keep.tile([P, 2, 2048], U8, name="as_raw", align_bytes=256)
         a_perm = [keep.tile([P, 2, 4, 256], U8, name="a_perm%d" % g, align_bytes=256) for g in range(NG)]
         as_perm = [keep.tile([P, 2, 4, 128], U8, name="as_perm%d" % g, align_bytes=256) for g in range(NG)]
@@ -51,8 +52,11 @@ def tile_mlem_pet_update_s4_kernel(tc, a_words, a_scales, x_words, x_scales, bac
         warm_out = keep.tile([P, 1], F32, name="warm_out")
 
         def load_a(lo, hi, queue):
-            if lo % 2 == 0:
-                queue.dma_start(out=a_raw[lo // 2][:].bitcast(I32), in_=a_words[:, :, 1024 * lo : 1024 * lo + 2048].rearrange("g p b -> p g b").bitcast(I32))
+            if lo == 2:
+                queue.dma_start(out=a_late[:].bitcast(I32), in_=a_words[:, :, 2048:4096].rearrange("g p b -> p g b").bitcast(I32))
+                return
+            for g in range(lo, hi):
+                queue.dma_start(out=a_raw[g][:].bitcast(I32), in_=a_words[:, :, 1024 * g : 1024 * g + 1024].rearrange("g p b -> p g b").bitcast(I32))
 
         def load_x(h, queue):
             queue.dma_start(out=x_sb[h][:].bitcast(I32), in_=x_words[:, :, 1024 * h : 1024 * h + 1024].rearrange("g p b -> p g b").bitcast(I32))
@@ -69,16 +73,18 @@ def tile_mlem_pet_update_s4_kernel(tc, a_words, a_scales, x_words, x_scales, bac
         def load_img(h):
             nc.sync.dma_start(out=img_sb[h][:], in_=img.rearrange("(m p) f -> p m f", p=P)[:, :, 512 * h : 512 * h + 512])
 
-        load_x(0, nc.gpsimd)
-        nc.vector.memset(as_raw[:].rearrange("p g n -> p (g n)").bitcast(I32), 0)
+        nc.vector.memset(as_raw[:, 0].bitcast(I32), 0)
+        nc.vector.memset(as_raw[:, 1].bitcast(I32), 0)
         nc.vector.memset(xs[:].rearrange("p g n -> p (g n)").bitcast(I32), 0)
-        load_scales(as_raw, a_scales, 0, nc.sync)
-        load_scales(as_raw, a_scales, 1, nc.sync)
-        load_a(0, 2, nc.sync)
-        for q in (2, 3):
-            load_scales(as_raw, a_scales, q, nc.sync)
+        load_a(0, 1, nc.sync)
         for q in range(4):
-            load_scales(xs, x_scales, q, nc.sync)
+            load_scales(as_raw, a_scales, q, nc.sync)
+        load_scales(xs, x_scales, 0, nc.sync)
+        load_scales(xs, x_scales, 1, nc.sync)
+        load_a(1, 2, nc.sync)
+        load_x(0, nc.gpsimd)
+        load_scales(xs, x_scales, 2, nc.sync)
+        load_scales(xs, x_scales, 3, nc.sync)
         nc.sync.dma_start(out=r_sb[:], in_=r.rearrange("(g p t) -> p g t", p=P, t=4))
         load_a(2, 4, nc.sync)
         nc.vector.memset(warm[:], 1.0)
@@ -107,7 +113,7 @@ def tile_mlem_pet_update_s4_kernel(tc, a_words, a_scales, x_words, x_scales, bac
             for k in range(2):
                 nc.vector.tensor_copy(
                     out=a_perm[g][:, k, lo:hi].rearrange("p t (c b) -> p t c b", b=2),
-                    in_=a_raw[g // 2][:, k, 1024 * (g % 2) : 1024 * (g % 2) + 1024].rearrange("p (c t b) -> p t c b", t=4, b=2)[:, lo:hi],
+                    in_=a_raw[g][:, k].rearrange("p (c t b) -> p t c b", t=4, b=2)[:, lo:hi],
                 )
 
         def permute_scales(g, ts=(0, 4)):
@@ -119,11 +125,8 @@ def tile_mlem_pet_update_s4_kernel(tc, a_words, a_scales, x_words, x_scales, bac
         permute_codes(0, (2, 4))
         permute_scales(0, (2, 4))
         permute_scales(1)
-        permute_codes(1)
         permute_scales(2)
         permute_scales(3)
-        permute_codes(2)
-        permute_codes(3)
 
         tiles1 = {}
         u = {}
@@ -210,22 +213,31 @@ def tile_mlem_pet_update_s4_kernel(tc, a_words, a_scales, x_words, x_scales, bac
 
         res = {}
 
-        def finish(c, m):
+        def finish(c, m, helped):
             w = WIDTHS[c]
             h, off = divmod(STARTS[c], 512)
-            single = w == 512 or (c == NCH - 1 and m >= 6)
+            single = w == 512 or (c == NCH - 1 and m >= 4)
             n = 1 if single else 2
             key = (c, m // n)
             if key not in res:
                 res[key] = [work.tile([P, n, w], F32, name="res%d" % n, align_bytes=256, bufs=(8 if n == 2 else 8)), 0]
             tile = res[key][0]
-            nc.vector.scalar_tensor_tensor(out=tile[:, m % n, :], in0=accs[c, m], scalar=rsens[:, m : m + 1], in1=img_sb[h][:, m, off : off + w], op0=ALU.mult, op1=ALU.mult)
+            pix = img_sb[h][:, m, off : off + w]
+            if helped:
+                mid = work.tile([P, w], F32, name="mid", align_bytes=256, bufs=2)
+                nc.scalar.activation(out=mid[:], in_=accs[c, m], func=ACT.Copy, scale=rsens[:, m : m + 1])
+                nc.gpsimd.tensor_tensor(out=tile[:, m % n, :], in0=mid[:], in1=pix, op=ALU.mult)
+            else:
+                nc.vector.scalar_tensor_tensor(out=tile[:, m % n, :], in0=accs[c, m], scalar=rsens[:, m : m + 1], in1=pix, op0=ALU.mult, op1=ALU.mult)
             res[key][1] += 1
             if res[key][1] == n:
                 m = m // n * n
                 nc.sync.dma_start(out=out.rearrange("(m p) f -> p m f", p=P)[:, m : m + n, STARTS[c] : STARTS[c] + w], in_=tile[:])
 
-        SEQ = [("T", "S1", 0, 0, 0), ("T", "S1", 0, 1, 1), ("S", "R", 0, 0), ("T", "S1", 0, 2, 2), ("S", "R", 0, 1), ("T", "S1", 0, 3, 3), ("S", "R", 0, 2), ("T", "S1", 1, 0, 4), ("S", "R", 0, 3), ("T", "S1", 1, 1, 5), ("S", "R", 1, 0), ("T", "S1", 1, 2, 6), ("S", "R", 1, 1), ("T", "S1", 1, 3, 7), ("V", "SQ", 0), ("S", "R", 1, 2), ("T", "S1", 2, 0, 0), ("S", "R", 1, 3), ("T", "S1", 2, 1, 1), ("S", "R", 2, 0), ("T", "S1", 2, 2, 2), ("S", "R", 2, 1), ("T", "S1", 2, 3, 3), ("V", "TT", 0), ("S", "SQ", 1), ("T", "S1", 3, 0, 4), ("T", "S1", 3, 1, 5), ("T", "S1", 3, 2, 6), ("T", "S1", 3, 3, 7), ("S", "R", 2, 2), ("V", "Q", 0), ("T", "S1", 4, 0, 0), ("S", "R", 2, 3), ("V", "TT", 1), ("T", "S1", 4, 1, 1), ("S", "R", 3, 0), ("T", "P", 0, 0, 0, 2), ("T", "P", 0, 1, 0, 3), ("S", "R", 3, 1), ("T", "P", 0, 2, 0, 4), ("S", "SQ", 2), ("T", "P", 0, 3, 0, 5), ("V", "Q", 1), ("T", "P", 0, 0, 1), ("T", "P", 0, 1, 1), ("T", "P", 0, 2, 1), ("S", "R", 3, 2), ("V", "TT", 2), ("T", "P", 0, 3, 1), ("S", "R", 3, 3), ("T", "S1", 5, 0, 6), ("S", "R", 4, 0), ("T", "P", 0, 4, 0, 7), ("S", "R", 4, 1), ("T", "P", 0, 4, 1), ("S", "SQ", 3), ("T", "S1", 5, 1, 0), ("V", "Q", 2), ("T", "P", 0, 0, 2), ("T", "P", 0, 1, 2), ("T", "P", 0, 2, 2), ("S", "R", 4, 2), ("V", "TT", 3), ("T", "P", 0, 3, 2), ("S", "R", 4, 3), ("T", "P", 0, 4, 2), ("S", "R", 5, 0), ("T", "S1", 6, 0, 1), ("S", "R", 5, 1), ("S", "SQ", 4), ("T", "S1", 6, 1, 6), ("S", "R", 5, 2), ("V", "TT", 4), ("S", "R", 5, 3), ("S", "R", 6, 0), ("T", "S1", 7, 0, 0), ("S", "R", 6, 1), ("V", "Q", 3), ("S", "SQ", 5), ("T", "S1", 7, 1, 1), ("V", "Q", 4), ("T", "P", 0, 0, 3), ("T", "P", 0, 1, 3), ("S", "R", 6, 2), ("V", "E", 0, 0), ("T", "P", 0, 2, 3), ("S", "R", 6, 3), ("T", "P", 0, 3, 3), ("V", "TT", 5), ("S", "R", 7, 0), ("T", "S1", 8, 0, 2), ("S", "R", 7, 1), ("S", "SQ", 6), ("T", "S1", 8, 1, 6), ("V", "E", 0, 1), ("T", "P", 0, 4, 3), ("T", "P", 0, 5, 0, 0), ("V", "Q", 5), ("S", "R", 7, 2), ("T", "P", 0, 5, 1), ("V", "TT", 6), ("T", "P", 0, 5, 2), ("S", "R", 7, 3), ("T", "S1", 9, 0, 3), ("S", "R", 8, 0), ("S", "R", 8, 1), ("T", "S1", 9, 1, 1), ("S", "SQ", 7), ("V", "E", 0, 2), ("T", "P", 0, 5, 3), ("V", "Q", 6), ("T", "P", 0, 6, 0, 2), ("V", "E", 0, 3), ("T", "P", 0, 6, 1), ("S", "R", 8, 2), ("T", "P", 0, 6, 2), ("S", "R", 8, 3), ("V", "TT", 7), ("T", "S1", 10, 0, 4), ("S", "R", 9, 0), ("S", "R", 9, 1), ("T", "S1", 10, 1, 5), ("S", "SQ", 8), ("V", "E", 0, 4), ("T", "P", 0, 6, 3), ("T", "P", 0, 7, 0, 6), ("V", "Q", 7), ("T", "P", 0, 7, 1), ("S", "R", 9, 2), ("T", "P", 0, 7, 2), ("V", "E", 0, 5), ("S", "R", 9, 3), ("T", "S1", 11, 0, 3), ("S", "R", 10, 0), ("V", "TT", 8), ("T", "P", 0, 7, 3), ("S", "R", 10, 1), ("T", "S1", 11, 1, 7), ("S", "SQ", 9), ("T", "P", 1, 0, 0, 1), ("V", "E", 0, 6), ("T", "P", 1, 0, 1), ("T", "P", 1, 0, 2), ("T", "P", 1, 0, 3), ("T", "P", 1, 1, 0, 0), ("V", "Q", 8), ("S", "R", 10, 2), ("T", "P", 1, 1, 1), ("T", "P", 1, 1, 2), ("V", "TT", 9), ("S", "R", 10, 3), ("T", "P", 1, 1, 3), ("T", "P", 1, 2, 0, 4), ("S", "R", 11, 0), ("T", "P", 1, 2, 1), ("T", "P", 1, 2, 2), ("T", "P", 1, 2, 3), ("S", "R", 11, 1), ("T", "P", 1, 3, 0, 2), ("T", "P", 1, 3, 1), ("S", "SQ", 10), ("T", "P", 1, 3, 2), ("V", "E", 0, 7), ("T", "P", 1, 3, 3), ("T", "P", 1, 4, 0, 5), ("T", "P", 1, 4, 1), ("T", "P", 1, 4, 2), ("V", "Q", 9), ("T", "P", 1, 4, 3), ("T", "P", 1, 5, 0, 3), ("V", "E", 1, 0), ("S", "R", 11, 2), ("T", "P", 1, 5, 1), ("T", "P", 1, 5, 2), ("V", "TT", 10), ("T", "P", 1, 5, 3), ("S", "R", 11, 3), ("T", "P", 1, 6, 0, 6), ("T", "P", 1, 6, 1), ("T", "P", 1, 6, 2), ("T", "P", 1, 6, 3), ("S", "SQ", 11), ("T", "P", 1, 7, 0, 1), ("T", "P", 1, 7, 1), ("T", "P", 1, 7, 2), ("V", "E", 1, 1), ("T", "P", 1, 7, 3), ("T", "P", 2, 0, 0, 7), ("V", "Q", 10), ("T", "P", 2, 0, 1), ("T", "P", 2, 1, 0, 0), ("V", "E", 1, 2), ("T", "P", 2, 1, 1), ("T", "P", 2, 0, 2), ("T", "P", 2, 1, 2), ("V", "TT", 11), ("T", "P", 2, 2, 0, 4), ("T", "P", 2, 2, 1), ("T", "P", 2, 2, 2), ("V", "E", 1, 3), ("V", "Q", 11), ("T", "P", 2, 3, 0, 2), ("T", "P", 2, 3, 1), ("V", "E", 1, 4), ("T", "P", 2, 3, 2), ("T", "P", 2, 0, 3), ("V", "E", 1, 5), ("T", "P", 2, 1, 3), ("T", "P", 2, 2, 3), ("V", "E", 1, 6), ("T", "P", 2, 3, 3), ("T", "P", 2, 4, 0, 5), ("T", "P", 2, 4, 1), ("V", "E", 1, 7), ("T", "P", 2, 4, 2), ("T", "P", 2, 4, 3), ("V", "E", 2, 0), ("T", "P", 2, 5, 0, 3), ("T", "P", 2, 5, 1), ("V", "E", 2, 1), ("T", "P", 2, 5, 2), ("T", "P", 2, 5, 3), ("V", "E", 2, 2), ("T", "P", 2, 6, 0, 6), ("T", "P", 2, 6, 1), ("V", "E", 2, 3), ("T", "P", 2, 6, 2), ("T", "P", 2, 6, 3), ("T", "P", 2, 7, 0, 1), ("V", "E", 2, 4), ("T", "P", 2, 7, 1), ("T", "P", 2, 7, 2), ("V", "E", 2, 5), ("T", "P", 2, 7, 3), ("V", "E", 2, 6), ("V", "E", 2, 7)]
+        junk = psum.tile([P, BANK], F32, name="bank7", bufs=1)
+        for i in range(4):
+            nc.tensor.matmul_mx(out=junk[:], lhsT=a_raw[0][:, i % 2, 0:256].bitcast(FP4X4), lhsT_scale=as_raw[:, i % 2, 0:128], rhs=a_raw[0][:, i % 2].bitcast(FP4X4), rhs_scale=as_raw[:, i % 2, 0:512], start=True, stop=True)
+        SEQ = [("T", "S1", 0, 0, 0), ("T", "S1", 0, 1, 1), ("S", "R", 0, 0), ("V", "PM", 1), ("T", "S1", 0, 2, 2), ("S", "R", 0, 1), ("T", "S1", 0, 3, 3), ("S", "R", 0, 2), ("V", "PM", 2), ("T", "S1", 1, 0, 4), ("S", "R", 0, 3), ("T", "S1", 1, 1, 5), ("S", "R", 1, 0), ("V", "PM", 3), ("T", "S1", 1, 2, 6), ("S", "R", 1, 1), ("T", "S1", 1, 3, 7), ("S", "R", 1, 2), ("V", "SQ", 0), ("T", "S1", 2, 0, 0), ("S", "R", 1, 3), ("T", "S1", 2, 1, 1), ("S", "R", 2, 0), ("T", "S1", 2, 2, 2), ("S", "R", 2, 1), ("T", "S1", 2, 3, 3), ("S", "R", 2, 2), ("T", "S1", 3, 0, 4), ("V", "TT", 0), ("S", "SQ", 1), ("T", "S1", 3, 1, 5), ("T", "S1", 3, 2, 6), ("T", "S1", 3, 3, 7), ("T", "S1", 4, 0, 0), ("V", "Q", 0), ("S", "R", 2, 3), ("T", "S1", 4, 1, 1), ("V", "TT", 1), ("S", "R", 3, 0), ("T", "P", 0, 0, 0, 2), ("T", "P", 0, 1, 0, 3), ("S", "R", 3, 1), ("T", "P", 0, 2, 0, 4), ("S", "R", 3, 2), ("T", "P", 0, 3, 0, 5), ("S", "SQ", 2), ("T", "P", 0, 4, 0, 6), ("V", "Q", 1), ("T", "P", 0, 0, 1), ("T", "P", 0, 1, 1), ("T", "P", 0, 2, 1), ("S", "R", 3, 3), ("T", "P", 0, 3, 1), ("V", "TT", 2), ("T", "P", 0, 4, 1), ("S", "R", 4, 0), ("T", "S1", 5, 0, 7), ("S", "R", 4, 1), ("S", "R", 4, 2), ("T", "S1", 5, 1, 0), ("S", "SQ", 3), ("V", "Q", 2), ("T", "P", 0, 0, 2), ("T", "P", 0, 1, 2), ("S", "R", 4, 3), ("T", "P", 0, 2, 2), ("V", "TT", 3), ("S", "R", 5, 0), ("T", "P", 0, 3, 2), ("S", "R", 5, 1), ("T", "S1", 6, 0, 1), ("S", "R", 5, 2), ("T", "S1", 6, 1, 7), ("S", "SQ", 4), ("T", "P", 0, 4, 2), ("S", "R", 5, 3), ("V", "TT", 4), ("S", "R", 6, 0), ("T", "S1", 7, 0, 0), ("S", "R", 6, 1), ("S", "R", 6, 2), ("T", "S1", 7, 1, 1), ("V", "Q", 3), ("S", "SQ", 5), ("V", "Q", 4), ("T", "P", 0, 0, 3), ("T", "P", 0, 1, 3), ("S", "R", 6, 3), ("V", "E", 0, 0), ("T", "P", 0, 2, 3), ("S", "R", 7, 0), ("T", "P", 0, 3, 3), ("V", "TT", 5), ("S", "R", 7, 1), ("T", "S1", 8, 0, 7), ("S", "R", 7, 2), ("T", "S1", 8, 1, 2), ("S", "SQ", 6), ("V", "E", 0, 1), ("T", "P", 0, 4, 3), ("T", "P", 0, 5, 0, 0), ("V", "Q", 5), ("S", "R", 7, 3), ("T", "P", 0, 5, 1), ("V", "TT", 6), ("T", "S1", 9, 0, 3), ("S", "R", 8, 0), ("S", "R", 8, 1), ("T", "S1", 9, 1, 1), ("S", "R", 8, 2), ("S", "SQ", 7), ("V", "E", 0, 2), ("T", "P", 0, 5, 2), ("T", "P", 0, 5, 3), ("V", "Q", 6), ("T", "P", 0, 6, 0, 7), ("V", "E", 0, 3), ("T", "P", 0, 6, 1), ("S", "R", 8, 3), ("T", "S1", 10, 0, 4), ("S", "R", 9, 0), ("V", "TT", 7), ("S", "R", 9, 1), ("T", "S1", 10, 1, 2), ("S", "R", 9, 2), ("S", "SQ", 8), ("T", "P", 0, 6, 2), ("V", "E", 0, 4), ("T", "P", 0, 6, 3), ("T", "P", 0, 7, 0, 5), ("T", "P", 0, 7, 1), ("V", "Q", 7), ("S", "R", 9, 3), ("T", "S1", 11, 0, 3), ("V", "TT", 8), ("S", "R", 10, 0), ("T", "P", 0, 7, 2), ("S", "R", 10, 1), ("T", "S1", 11, 1, 6), ("S", "R", 10, 2), ("V", "E", 0, 5), ("S", "SQ", 9), ("T", "P", 0, 7, 3), ("T", "P", 1, 0, 0, 1), ("V", "Q", 8), ("T", "P", 1, 0, 1), ("T", "P", 1, 0, 2), ("V", "E", 0, 6), ("T", "P", 1, 0, 3), ("T", "P", 1, 1, 0, 4), ("S", "R", 10, 3), ("T", "P", 1, 1, 1), ("T", "P", 1, 1, 2), ("S", "R", 11, 0), ("T", "P", 1, 1, 3), ("V", "TT", 9), ("T", "P", 1, 2, 0, 0), ("S", "R", 11, 1), ("T", "P", 1, 2, 1), ("T", "P", 1, 2, 2), ("T", "P", 1, 2, 3), ("S", "R", 11, 2), ("T", "P", 1, 3, 0, 2), ("T", "P", 1, 3, 1), ("S", "SQ", 10), ("T", "P", 1, 3, 2), ("V", "E", 0, 7), ("T", "P", 1, 3, 3), ("T", "P", 1, 4, 0, 7), ("T", "P", 1, 4, 1), ("T", "P", 1, 4, 2), ("V", "Q", 9), ("T", "P", 1, 4, 3), ("T", "P", 1, 5, 0, 3), ("S", "R", 11, 3), ("T", "P", 1, 5, 1), ("V", "E", 1, 0), ("T", "P", 1, 5, 2), ("T", "P", 1, 5, 3), ("V", "TT", 10), ("T", "P", 1, 6, 0, 5), ("S", "SQ", 11), ("T", "P", 1, 6, 1), ("T", "P", 1, 6, 2), ("T", "P", 1, 6, 3), ("T", "P", 1, 7, 0, 6), ("T", "P", 1, 7, 1), ("T", "P", 1, 7, 2), ("T", "P", 1, 7, 3), ("V", "E", 1, 1), ("T", "P", 2, 0, 0, 1), ("T", "P", 2, 0, 1), ("V", "Q", 10), ("T", "P", 2, 1, 0, 4), ("T", "P", 2, 1, 1), ("V", "TT", 11), ("T", "P", 2, 0, 2), ("T", "P", 2, 1, 2), ("V", "E", 1, 2), ("V", "Q", 11), ("T", "P", 2, 2, 0, 0), ("T", "P", 2, 2, 1), ("V", "E", 1, 3), ("T", "P", 2, 2, 2), ("T", "P", 2, 0, 3), ("V", "E", 1, 4), ("T", "P", 2, 1, 3), ("T", "P", 2, 2, 3), ("V", "E", 1, 5), ("T", "P", 2, 3, 0, 2), ("T", "P", 2, 3, 1), ("T", "P", 2, 3, 2), ("V", "E", 1, 6), ("T", "P", 2, 3, 3), ("T", "P", 2, 4, 0, 7), ("V", "E", 1, 7), ("T", "P", 2, 4, 1), ("T", "P", 2, 4, 2), ("V", "E", 2, 0), ("T", "P", 2, 4, 3), ("T", "P", 2, 5, 0, 3), ("V", "E", 2, 1), ("T", "P", 2, 5, 1), ("T", "P", 2, 5, 2), ("T", "P", 2, 5, 3), ("V", "E", 2, 2), ("T", "P", 2, 6, 0, 5), ("T", "P", 2, 6, 1), ("V", "E", 2, 3), ("T", "P", 2, 6, 2), ("T", "P", 2, 6, 3), ("V", "E", 2, 4), ("T", "P", 2, 7, 0, 6), ("T", "P", 2, 7, 1), ("V", "E", 2, 5), ("T", "P", 2, 7, 2), ("T", "P", 2, 7, 3), ("V", "E", 2, 6), ("V", "E", 2, 7)]
         first = True
         for ev in SEQ:
             e, kind, args = ev[0], ev[1], ev[2:]
@@ -242,6 +254,8 @@ def tile_mlem_pet_update_s4_kernel(tc, a_words, a_scales, x_words, x_scales, bac
                 inverse_root(*args)
             elif kind == "SQ":
                 square(args[0], e == "V")
+            elif kind == "PM":
+                permute_codes(args[0])
             elif kind == "TT":
                 ratio(args[0])
             elif kind == "Q":
@@ -252,4 +266,4 @@ def tile_mlem_pet_update_s4_kernel(tc, a_words, a_scales, x_words, x_scales, bac
                     nc.vector.reciprocal(out=rsens[:], in_=turned[:, 0:NM])
                 quantize(args[0])
             else:
-                finish(*args)
+                finish(args[0], args[1], kind == "ES")

from contextlib import ExitStack

import concourse.mybir as mybir
from concourse.masks import make_identity

V, B, F = 1024, 2048, 1024
FLOPS = 2 * V * B * F * 2

F32 = mybir.dt.float32
BF16 = mybir.dt.bfloat16
U32 = mybir.dt.uint32
I32 = mybir.dt.int32
U8 = mybir.dt.uint8
FP8X4 = mybir.dt.float8_e4m3fn_x4
FP4X4 = mybir.dt.float4_e2m1fn_x4
ACT = mybir.ActivationFunctionType
ALU = mybir.AluOpType

P = 128
NG = 4
NM = 8
BANK = 512
WIDTHS = [512,256,256]
STARTS = [sum(WIDTHS[:i]) for i in range(len(WIDTHS))]
NCH = len(WIDTHS)


def tile_mlem_pet_update_s4_kernel(tc, a_words, a_scales, x_words, x_scales, back_words, back_scales, y, r, img, sens, out):
    nc = tc.nc
    with ExitStack() as ctx:
        keep = ctx.enter_context(tc.tile_pool(name="keep", bufs=1))
        work = ctx.enter_context(tc.tile_pool(name="work", bufs=3))
        psum = ctx.enter_context(tc.psum_pool(name="psum", bufs=4))
        ctx.enter_context(tc.manual_schedule())

        x_sb = [keep.tile([P, 2, 1024], U8, name="x_sb%d" % h, align_bytes=256) for h in range(2)]
        xs = keep.tile([P, 2, 1024], U8, name="xs", align_bytes=256)
        a_late = keep.tile([P, 2, 2048], U8, name="a_late", align_bytes=256)
        a_raw = [keep.tile([P, 2, 1024], U8, name="a_raw%d" % g, align_bytes=256) for g in range(2)] + [a_late[:, :, 0:1024], a_late[:, :, 1024:2048]]
        as_raw = keep.tile([P, 2, 2048], U8, name="as_raw", align_bytes=256)
        a_perm = [keep.tile([P, 2, 4, 256], U8, name="a_perm%d" % g, align_bytes=256) for g in range(NG)]
        as_perm = [keep.tile([P, 2, 4, 128], U8, name="as_perm%d" % g, align_bytes=256) for g in range(NG)]
        back_sb = [keep.tile([P, 4096], U8, name="back%d" % g, align_bytes=256) for g in range(NG)]
        bs = keep.tile([P, 1024], U8, name="bs", align_bytes=256)
        y_sb = [[keep.tile([P, 4, 512], BF16, name="y%d_%d" % (g, h), align_bytes=256) for h in range(2)] for g in range(NG)]
        img_sb = [keep.tile([P, NM, 512], BF16, name="img%d" % h, align_bytes=256) for h in range(2)]
        r_sb = keep.tile([P, 4, 4], BF16, name="r_sb")
        sens_rows = keep.tile([P, P], BF16, name="sens_rows", align_bytes=256)
        ident = keep.tile([P, P], BF16, name="ident", align_bytes=256)
        rsens = keep.tile([P, NM], F32, name="rsens")
        warm = keep.tile([P, 1], F32, name="warm")
        warm_out = keep.tile([P, 1], F32, name="warm_out")

        def load_a(lo, hi, queue):
            if lo == 2:
                queue.dma_start(out=a_late[:].bitcast(I32), in_=a_words[:, :, 2048:4096].rearrange("g p b -> p g b").bitcast(I32))
                return
            for g in range(lo, hi):
                queue.dma_start(out=a_raw[g][:].bitcast(I32), in_=a_words[:, :, 1024 * g : 1024 * g + 1024].rearrange("g p b -> p g b").bitcast(I32))

        def load_x(h, queue):
            queue.dma_start(out=x_sb[h][:].bitcast(I32), in_=x_words[:, :, 1024 * h : 1024 * h + 1024].rearrange("g p b -> p g b").bitcast(I32))

        def load_scales(tile, src, q, queue):
            queue.dma_start(out=tile[32 * q : 32 * q + 4, :, :].bitcast(I32), in_=src[:, 4 * q : 4 * q + 4, :].rearrange("g r n -> r g n").bitcast(I32))

        def load_y(g, h):
            nc.sync.dma_start(out=y_sb[g][h][:], in_=y.rearrange("(g p t) f -> g p t f", p=P, t=4)[g][:, :, 512 * h : 512 * h + 512])

        def load_back(g):
            nc.sync.dma_start(out=back_sb[g][:].bitcast(I32), in_=back_words[g].rearrange("p n t -> p (n t)").bitcast(I32))

        def load_img(h):
            nc.sync.dma_start(out=img_sb[h][:], in_=img.rearrange("(m p) f -> p m f", p=P)[:, :, 512 * h : 512 * h + 512])

        nc.vector.memset(as_raw[:, 0].bitcast(I32), 0)
        nc.vector.memset(as_raw[:, 1].bitcast(I32), 0)
        nc.vector.memset(xs[:].rearrange("p g n -> p (g n)").bitcast(I32), 0)
        load_a(0, 1, nc.sync)
        for q in range(4):
            load_scales(as_raw, a_scales, q, nc.sync)
        load_scales(xs, x_scales, 0, nc.sync)
        load_scales(xs, x_scales, 1, nc.sync)
        load_a(1, 2, nc.sync)
        load_x(0, nc.gpsimd)
        load_scales(xs, x_scales, 2, nc.sync)
        load_scales(xs, x_scales, 3, nc.sync)
        nc.sync.dma_start(out=r_sb[:], in_=r.rearrange("(g p t) -> p g t", p=P, t=4))
        load_a(2, 4, nc.sync)
        nc.vector.memset(warm[:], 1.0)
        nc.scalar.activation(out=warm_out[:], in_=warm[:], func=ACT.Abs_reciprocal_sqrt)
        nc.gpsimd.memset(sens_rows[:], 0.0)
        nc.gpsimd.memset(bs[:].bitcast(I32), 0)
        make_identity(nc, ident[:])
        load_y(0, 0)
        load_y(1, 0)
        nc.sync.dma_start(out=sens_rows[0:NM, :], in_=sens.rearrange("(m p) -> m p", p=P))
        for q in range(4):
            nc.sync.dma_start(out=bs[32 * q : 32 * q + 16, :].bitcast(I32), in_=back_scales[:, 4 * q : 4 * q + 4, :].bitcast(I32))
        load_back(0)
        load_y(2, 0)
        load_back(1)
        load_y(3, 0)
        load_x(1, nc.sync)
        load_back(2)
        load_back(3)
        load_img(0)
        for g in range(NG):
            load_y(g, 1)
        load_img(1)
        def permute_codes(g, ts=(0, 4)):
            lo, hi = ts
            for k in range(2):
                nc.vector.tensor_copy(
                    out=a_perm[g][:, k, lo:hi].rearrange("p t (c b) -> p t c b", b=2),
                    in_=a_raw[g][:, k].rearrange("p (c t b) -> p t c b", t=4, b=2)[:, lo:hi],
                )

        def permute_scales(g, ts=(0, 4)):
            lo, hi = ts
            nc.vector.tensor_copy(out=as_perm[g][:, :, lo:hi], in_=as_raw[:, :, 512 * g : 512 * g + 512].rearrange("p k (c t) -> p k t c", t=4)[:, :, lo:hi])

        permute_codes(0, (0, 2))
        permute_scales(0, (0, 2))
        permute_codes(0, (2, 4))
        permute_scales(0, (2, 4))
        permute_scales(1)
        permute_scales(2)
        permute_scales(3)

        tiles1 = {}
        u = {}
        rec = {}
        codes = {}
        planes = {}
        quant_in = {}

        def stage1(j, b, k_bank):
            c, g = divmod(j, NG)
            w = WIDTHS[c]
            h, off = divmod(STARTS[c], 512)
            per = BANK // w
            bank = psum.tile([P, per, w], F32, name="bank%d" % k_bank, bufs=1)
            for e in range(per):
                t = per * b + e
                tiles1[j, t] = bank[:, e, :]
                for k in range(2):
                    nc.tensor.matmul_mx(
                        out=bank[:, e, :],
                        lhsT=a_perm[g][:, k, t, :].bitcast(FP4X4),
                        lhsT_scale=as_perm[g][:, k, t, :],
                        rhs=x_sb[h][:, k, 2 * off : 2 * off + 2 * w].bitcast(FP4X4),
                        rhs_scale=xs[:, k, STARTS[c] : STARTS[c] + w],
                        start=(k == 0),
                        stop=(k == 1),
                    )

        def inverse_root(j, t):
            c, g = divmod(j, NG)
            if t == 0:
                u[j] = work.tile([P, 4, WIDTHS[c]], F32, name="u", align_bytes=256)
            nc.scalar.activation(out=u[j][:, t, :], in_=tiles1[j, t], func=ACT.Abs_reciprocal_sqrt, bias=r_sb[:, g, t : t + 1])

        LASTJ = NCH * NG - 1

        def parts(j):
            n = 1 if j == LASTJ else 1
            w = WIDTHS[j // NG]
            return [(i * w // n, (i + 1) * w // n) for i in range(n)]

        def square(j, on_vector):
            rec[j] = work.tile([P, 4, WIDTHS[j // NG]], F32, name="rec", align_bytes=256)
            for lo, hi in parts(j):
                if on_vector:
                    nc.vector.tensor_tensor(out=rec[j][:, :, lo:hi], in0=u[j][:, :, lo:hi], in1=u[j][:, :, lo:hi], op=ALU.mult)
                else:
                    nc.scalar.activation(out=rec[j][:, :, lo:hi], in_=u[j][:, :, lo:hi], func=ACT.Square)

        def ratio(j):
            c, g = divmod(j, NG)
            w = WIDTHS[c]
            quant_in[j] = work.tile([P, 4 * w], BF16, name="quant_in", align_bytes=256)
            for lo, hi in parts(j):
                for a in range(lo, hi, 512):
                    h, off = divmod(STARTS[c] + a, 512)
                    n = min(hi - a, 512 - off)
                    nc.vector.tensor_tensor(
                        out=quant_in[j][:, 4 * a : 4 * (a + n)].rearrange("p (c i t) -> p c t i", i=4, t=4),
                        in0=rec[j][:, :, a : a + n].rearrange("p t (c i) -> p c t i", i=4),
                        in1=y_sb[g][h][:, :, off : off + n].rearrange("p t (c i) -> p c t i", i=4),
                        op=ALU.mult,
                    )

        def quantize(j):
            w = WIDTHS[j // NG]
            codes[j] = keep.tile([P, w], U32, name="codes%d" % j, align_bytes=256)
            planes[j] = keep.tile([P, w], U8, name="plane%d" % j, align_bytes=256)
            for lo, hi in parts(j):
                nc.vector.quantize_mx(out=codes[j][:, lo:hi].bitcast(FP8X4), scales=planes[j][:, lo:hi], in_=quant_in[j][:, 4 * lo : 4 * hi])

        accs = {}

        def stage2_pass(m, c, g):
            nc.tensor.matmul_mx(
                out=accs[c, m],
                lhsT=back_sb[g][:, 512 * m : 512 * m + 512].bitcast(FP8X4),
                lhsT_scale=bs[4 * g : P, P * m : P * m + P],
                rhs=codes[NG * c + g][:].bitcast(FP8X4),
                rhs_scale=planes[NG * c + g][:],
                start=(g == 0),
                stop=(g == NG - 1),
            )

        res = {}

        def finish(c, m, helped):
            w = WIDTHS[c]
            h, off = divmod(STARTS[c], 512)
            single = w == 512 or (c == NCH - 1 and m >= 4)
            n = 1 if single else 2
            key = (c, m // n)
            if key not in res:
                res[key] = [work.tile([P, n, w], F32, name="res%d" % n, align_bytes=256, bufs=(8 if n == 2 else 8)), 0]
            tile = res[key][0]
            pix = img_sb[h][:, m, off : off + w]
            if helped:
                mid = work.tile([P, w], F32, name="mid", align_bytes=256, bufs=2)
                nc.scalar.activation(out=mid[:], in_=accs[c, m], func=ACT.Copy, scale=rsens[:, m : m + 1])
                nc.gpsimd.tensor_tensor(out=tile[:, m % n, :], in0=mid[:], in1=pix, op=ALU.mult)
            else:
                nc.vector.scalar_tensor_tensor(out=tile[:, m % n, :], in0=accs[c, m], scalar=rsens[:, m : m + 1], in1=pix, op0=ALU.mult, op1=ALU.mult)
            res[key][1] += 1
            if res[key][1] == n:
                m = m // n * n
                nc.sync.dma_start(out=out.rearrange("(m p) f -> p m f", p=P)[:, m : m + n, STARTS[c] : STARTS[c] + w], in_=tile[:])

        junk = psum.tile([P, BANK], F32, name="bank7", bufs=1)
        for i in range(4):
            nc.tensor.matmul_mx(out=junk[:], lhsT=a_raw[0][:, i % 2, 0:256].bitcast(FP4X4), lhsT_scale=as_raw[:, i % 2, 0:128], rhs=a_raw[0][:, i % 2].bitcast(FP4X4), rhs_scale=as_raw[:, i % 2, 0:512], start=True, stop=True)
        SEQ = [("T", "S1", 0, 0, 0), ("T", "S1", 0, 1, 1), ("S", "R", 0, 0), ("V", "PM", 1), ("T", "S1", 0, 2, 2), ("S", "R", 0, 1), ("T", "S1", 0, 3, 3), ("S", "R", 0, 2), ("V", "PM", 2), ("T", "S1", 1, 0, 4), ("S", "R", 0, 3), ("T", "S1", 1, 1, 5), ("S", "R", 1, 0), ("V", "PM", 3), ("T", "S1", 1, 2, 6), ("S", "R", 1, 1), ("T", "S1", 1, 3, 7), ("S", "R", 1, 2), ("V", "SQ", 0), ("T", "S1", 2, 0, 0), ("S", "R", 1, 3), ("T", "S1", 2, 1, 1), ("S", "R", 2, 0), ("T", "S1", 2, 2, 2), ("S", "R", 2, 1), ("T", "S1", 2, 3, 3), ("S", "R", 2, 2), ("T", "S1", 3, 0, 4), ("V", "TT", 0), ("S", "SQ", 1), ("T", "S1", 3, 1, 5), ("T", "S1", 3, 2, 6), ("T", "S1", 3, 3, 7), ("T", "S1", 4, 0, 0), ("V", "Q", 0), ("S", "R", 2, 3), ("T", "S1", 4, 1, 1), ("V", "TT", 1), ("S", "R", 3, 0), ("T", "P", 0, 0, 0, 2), ("T", "P", 0, 1, 0, 3), ("S", "R", 3, 1), ("T", "P", 0, 2, 0, 4), ("S", "R", 3, 2), ("T", "P", 0, 3, 0, 5), ("S", "SQ", 2), ("T", "P", 0, 4, 0, 6), ("V", "Q", 1), ("T", "P", 0, 0, 1), ("T", "P", 0, 1, 1), ("T", "P", 0, 2, 1), ("S", "R", 3, 3), ("T", "P", 0, 3, 1), ("V", "TT", 2), ("T", "P", 0, 4, 1), ("S", "R", 4, 0), ("T", "S1", 5, 0, 7), ("S", "R", 4, 1), ("S", "R", 4, 2), ("T", "S1", 5, 1, 0), ("S", "SQ", 3), ("V", "Q", 2), ("T", "P", 0, 0, 2), ("T", "P", 0, 1, 2), ("S", "R", 4, 3), ("T", "P", 0, 2, 2), ("V", "TT", 3), ("S", "R", 5, 0), ("T", "P", 0, 3, 2), ("S", "R", 5, 1), ("T", "S1", 6, 0, 1), ("S", "R", 5, 2), ("T", "S1", 6, 1, 7), ("S", "SQ", 4), ("T", "P", 0, 4, 2), ("S", "R", 5, 3), ("V", "TT", 4), ("S", "R", 6, 0), ("T", "S1", 7, 0, 0), ("S", "R", 6, 1), ("S", "R", 6, 2), ("T", "S1", 7, 1, 1), ("V", "Q", 3), ("S", "SQ", 5), ("V", "Q", 4), ("T", "P", 0, 0, 3), ("T", "P", 0, 1, 3), ("S", "R", 6, 3), ("V", "E", 0, 0), ("T", "P", 0, 2, 3), ("S", "R", 7, 0), ("T", "P", 0, 3, 3), ("V", "TT", 5), ("S", "R", 7, 1), ("T", "S1", 8, 0, 7), ("S", "R", 7, 2), ("T", "S1", 8, 1, 2), ("S", "SQ", 6), ("V", "E", 0, 1), ("T", "P", 0, 4, 3), ("T", "P", 0, 5, 0, 0), ("V", "Q", 5), ("S", "R", 7, 3), ("T", "P", 0, 5, 1), ("V", "TT", 6), ("T", "S1", 9, 0, 3), ("S", "R", 8, 0), ("S", "R", 8, 1), ("T", "S1", 9, 1, 1), ("S", "R", 8, 2), ("S", "SQ", 7), ("V", "E", 0, 2), ("T", "P", 0, 5, 2), ("T", "P", 0, 5, 3), ("V", "Q", 6), ("T", "P", 0, 6, 0, 7), ("V", "E", 0, 3), ("T", "P", 0, 6, 1), ("S", "R", 8, 3), ("T", "S1", 10, 0, 4), ("S", "R", 9, 0), ("V", "TT", 7), ("S", "R", 9, 1), ("T", "S1", 10, 1, 2), ("S", "R", 9, 2), ("S", "SQ", 8), ("T", "P", 0, 6, 2), ("V", "E", 0, 4), ("T", "P", 0, 6, 3), ("T", "P", 0, 7, 0, 5), ("T", "P", 0, 7, 1), ("V", "Q", 7), ("S", "R", 9, 3), ("T", "S1", 11, 0, 3), ("V", "TT", 8), ("S", "R", 10, 0), ("T", "P", 0, 7, 2), ("S", "R", 10, 1), ("T", "S1", 11, 1, 6), ("S", "R", 10, 2), ("V", "E", 0, 5), ("S", "SQ", 9), ("T", "P", 0, 7, 3), ("T", "P", 1, 0, 0, 1), ("V", "Q", 8), ("T", "P", 1, 0, 1), ("T", "P", 1, 0, 2), ("V", "E", 0, 6), ("T", "P", 1, 0, 3), ("T", "P", 1, 1, 0, 4), ("S", "R", 10, 3), ("T", "P", 1, 1, 1), ("T", "P", 1, 1, 2), ("S", "R", 11, 0), ("T", "P", 1, 1, 3), ("V", "TT", 9), ("T", "P", 1, 2, 0, 0), ("S", "R", 11, 1), ("T", "P", 1, 2, 1), ("T", "P", 1, 2, 2), ("T", "P", 1, 2, 3), ("S", "R", 11, 2), ("T", "P", 1, 3, 0, 2), ("T", "P", 1, 3, 1), ("S", "SQ", 10), ("T", "P", 1, 3, 2), ("V", "E", 0, 7), ("T", "P", 1, 3, 3), ("T", "P", 1, 4, 0, 7), ("T", "P", 1, 4, 1), ("T", "P", 1, 4, 2), ("V", "Q", 9), ("T", "P", 1, 4, 3), ("T", "P", 1, 5, 0, 3), ("S", "R", 11, 3), ("T", "P", 1, 5, 1), ("V", "E", 1, 0), ("T", "P", 1, 5, 2), ("T", "P", 1, 5, 3), ("V", "TT", 10), ("T", "P", 1, 6, 0, 5), ("S", "SQ", 11), ("T", "P", 1, 6, 1), ("T", "P", 1, 6, 2), ("T", "P", 1, 6, 3), ("T", "P", 1, 7, 0, 6), ("T", "P", 1, 7, 1), ("T", "P", 1, 7, 2), ("T", "P", 1, 7, 3), ("V", "E", 1, 1), ("T", "P", 2, 0, 0, 1), ("T", "P", 2, 0, 1), ("V", "Q", 10), ("T", "P", 2, 1, 0, 4), ("T", "P", 2, 1, 1), ("V", "TT", 11), ("T", "P", 2, 0, 2), ("T", "P", 2, 1, 2), ("V", "E", 1, 2), ("V", "Q", 11), ("T", "P", 2, 2, 0, 0), ("T", "P", 2, 2, 1), ("V", "E", 1, 3), ("T", "P", 2, 2, 2), ("T", "P", 2, 0, 3), ("V", "E", 1, 4), ("T", "P", 2, 1, 3), ("T", "P", 2, 2, 3), ("V", "E", 1, 5), ("T", "P", 2, 3, 0, 2), ("T", "P", 2, 3, 1), ("T", "P", 2, 3, 2), ("V", "E", 1, 6), ("T", "P", 2, 3, 3), ("T", "P", 2, 4, 0, 7), ("V", "E", 1, 7), ("T", "P", 2, 4, 1), ("T", "P", 2, 4, 2), ("V", "E", 2, 0), ("T", "P", 2, 4, 3), ("T", "P", 2, 5, 0, 3), ("V", "E", 2, 1), ("T", "P", 2, 5, 1), ("T", "P", 2, 5, 2), ("T", "P", 2, 5, 3), ("V", "E", 2, 2), ("T", "P", 2, 6, 0, 5), ("T", "P", 2, 6, 1), ("V", "E", 2, 3), ("T", "P", 2, 6, 2), ("T", "P", 2, 6, 3), ("V", "E", 2, 4), ("T", "P", 2, 7, 0, 6), ("T", "P", 2, 7, 1), ("V", "E", 2, 5), ("T", "P", 2, 7, 2), ("T", "P", 2, 7, 3), ("V", "E", 2, 6), ("V", "E", 2, 7)]
        first = True
        for ev in SEQ:
            e, kind, args = ev[0], ev[1], ev[2:]
            if kind == "S1":
                stage1(*args)
            elif kind == "P":
                c, m, g = args[:3]
                if first:
                    first = False
                if g == 0:
                    accs[c, m] = psum.tile([P, BANK], F32, name="bank%d" % args[3], bufs=1)[:, 0 : WIDTHS[c]]
                stage2_pass(m, c, g)
            elif kind == "R":
                inverse_root(*args)
            elif kind == "SQ":
                square(args[0], e == "V")
            elif kind == "PM":
                permute_codes(args[0])
            elif kind == "TT":
                ratio(args[0])
            elif kind == "Q":
                if args[0] == 0:
                    b0 = [ev2[5] for ev2 in SEQ if len(ev2) == 6][0]
                    turned = psum.tile([P, P], BF16, name="bank%d" % b0, bufs=1)
                    nc.tensor.transpose(turned[:], sens_rows[:], ident[:])
                    nc.vector.reciprocal(out=rsens[:], in_=turned[:, 0:NM])
                quantize(args[0])
            else:
                finish(args[0], args[1], kind == "ES")
